import numpy as np, ml_dtypes
CORES = [48,51,52,55]
N = 4
import mx_ref
BF = ml_dtypes.bfloat16
def gentries(a):
    return np.ascontiguousarray(a.reshape(8, 16, -1).transpose(0, 2, 1)).reshape(8, -1)
def gtable(e):
    e = np.asarray(e); return np.ascontiguousarray(e.reshape(8, -1, 16).transpose(0, 2, 1)).reshape(128, -1).astype(np.int32)
def gcols(t, e):
    v = np.concatenate([t.reshape(8, 16, -1, 4), np.zeros((8, 16, 1, 4), BF)], axis=2)
    return np.ascontiguousarray(np.stack([v[g][:, e[g]] for g in range(8)])).reshape(128, -1)
def tile(rs):
    return np.stack(rs, axis=2).reshape(128, -1).astype(BF)
def pick(q, e):
    c = np.concatenate([q[0].reshape(128, -1, 4), np.zeros((128, 1, 4), np.uint8)], axis=1); s = np.concatenate([q[1], np.ones((16, 1), np.uint8)], axis=1)
    return (np.ascontiguousarray(c[:, e].reshape(128, -1)), np.ascontiguousarray(s[:, e]))
def join(*qs):
    return (np.concatenate([q[0] for q in qs], axis=1), np.concatenate([q[1] for q in qs], axis=1))
def put(q, e, v):
    c, s = q[0].reshape(128, -1, 4).copy(), q[1].copy(); c[:, e] = v[0].reshape(128, -1, 4); s[:, e] = v[1]
    return (c.reshape(128, -1), s)
def pk(c, s):
    return (np.ascontiguousarray(c), mx_ref.live(s))
def emit(q):
    return q[0], q[1]
def packed(v, rng):
    q = [mx_ref.quantize(np.ascontiguousarray(v[r])) for r in range(N)]
    return np.stack([a for a, b in q]), np.stack([mx_ref.plane(b, rng) for a, b in q])
def values_of_codes():
    e, c = np.zeros((128, 128, 4), np.float32), np.zeros((128, 2, 4), np.uint8)
    e[np.arange(128), np.arange(128), 0] = 1
    c[:127, :, 0] = np.arange(256).reshape(2, 128).T[:127]
    return mx_ref.matmul(mx_ref.quantize(e.reshape(128, 512).astype(BF)), (c.reshape(128, 8), np.full((16, 2), 127, np.uint8))).T.reshape(-1).astype(np.float64)
CODE_VALUE, SCALE_VALUE = values_of_codes(), 2.0 ** (np.arange(256) - 127.0)
def decode(q):
    return (CODE_VALUE[q[0]].reshape(16, 8, -1, 4) * SCALE_VALUE[q[1]][:, None, :, None] + 0.0).reshape(128, -1).astype(np.float32)
def f(rng, *shape):
    return mx_ref.flush((rng.standard_normal(shape, dtype=np.float32) * np.exp2(rng.integers(-2, 3, shape[:-1] + (1,)))).astype(BF))
def wide(rng, *shape, cols=0):
    v = rng.standard_normal(shape, dtype=np.float32) * np.exp2(rng.integers(-12, 13, shape)).astype(np.float32)
    if cols: v *= np.repeat(np.exp2(rng.integers(-cols, cols + 1, shape[:-2] + (1, shape[-1] // 4))) * (rng.random(shape[:-2] + (1, shape[-1] // 4)) > 0.0625), 4, axis=-1).astype(np.float32)
    return mx_ref.flush(v.astype(BF))
C, H, R = 384, 160, 3
def big(v):
    v = v.astype(np.float32)
    v[np.abs(v) < np.float32(2.0 ** -16)] = 0
    return v.astype(BF)
def numbers_of(rng):
    return {"x": big(f(rng, N, 128, 4 * C)), "u": np.array(f(rng, N, 128, 512)), "v": np.array(f(rng, N, 128, 512))}
def layers(rng, still=[]):
    w = big(f(rng, N, 128, 2048)).reshape(N, 8, 16, 4, 8, 16, 4)
    for i in still: w[:, :, :, :, :, i] = 0
    return w
def weights(rng, w):
    c, s = packed(np.ascontiguousarray(w).reshape(N, 128, 2048), rng)
    return {"wc": c, "ws": s}
def holes(rng):
    return np.sort(np.argsort(rng.random((N, 8, C - 1)), axis=2)[:, :, :H], axis=2)
def throws(rng, a):
    free = np.ones((N, 8, 2 * C), bool)
    free[:, :, C:] = False
    np.put_along_axis(free, a, False, axis=2)
    np.put_along_axis(free, C + np.roll(a, -1, axis=0), True, axis=2)
    e = np.zeros((N, 8, C), np.int64)
    for i in range(C - 1, -1, -1):
        k = (0.5 + rng.random((N, 8, C))) * free[:, :, i:i + C]
        k[:, :, C - 1] = 2.0 * free[:, :, i + C - 1]
        e[:, :, i] = i + np.argmax(k, axis=2)
        np.put_along_axis(free, e[:, :, i:i + 1], False, axis=2)
    return e
def lists(e):
    return np.stack([gtable(e[r]) for r in range(N)])
def meet(rng, e):
    used, out = [False] * C, []
    e = e.tolist()
    for i, k in zip(rng.permutation(C).tolist(), rng.integers(0, 4, C).tolist()):
        j = e[i] + (0, 1, 1 - C, -C)[k]
        if 0 <= j < C and j != i and not used[i] and not used[j]:
            used[i] = used[j] = True
            out += [i, j]
    return np.array(out + [int(i) for i in rng.permutation(C) if not used[i]])
def setup_inputs(rng):
    return {**numbers_of(rng), "p": lists(throws(rng, holes(rng))), **weights(rng, layers(rng))}
def setup_inputs_ties(rng):
    d = numbers_of(rng)
    o = rng.permutation(N)
    x = d["x"].reshape(N, 8, 16, C, 4)
    k = rng.integers(0, 3, (N, 8, C))
    k[o[2]] = 1
    x[:, :, 0] = 0
    x[:, :, 0, :, 0] = k.astype(np.float32).astype(BF)
    u = d["u"].reshape(N, 128, 128, 4)
    u[:, :, ::16] = 0
    for r in range(N):
        for h in range(0, 128, 16): u[r, h, h, 0] = 0.0 if r == o[0] else -1.0 if r == o[1] else 1.0
    return {"x": x.reshape(N, 128, 4 * C), "u": u.reshape(N, 128, 512), "v": d["v"], "p": lists(throws(rng, holes(rng))), **weights(rng, layers(rng, [0]))}
def setup_inputs_near(rng):
    d = numbers_of(rng)
    o = rng.permutation(N) % 4
    low = rng.permutation(8)[:4]
    x = d["x"].astype(np.float32).reshape(N, 8, 16, C, 4)
    u = d["u"].reshape(N, 128, 128, 4)
    x[:, :, 0] = 0
    x[:, :, 8:] = 0
    u[:, :, ::16] = 0
    for r in range(N):
        k = 1.0 if o[r] == 0 else 2.0 ** -30
        if o[r] < 3:
            s = rng.integers(0, 16, (8, C))
            x[r, :, 8] = ((s[:, :, None] >> np.arange(4)) & 1) * np.exp2(np.arange(4) - 23.0)
        else:
            x[r, :, 8, :, 0] = rng.integers(8, 16, (8, C)) * rng.choice([-1.0, 1.0], (8, C)) * 2.0 ** -27
            for g in low: x[r, g, 8:10, :, 0] = rng.integers(8, 15, (2, C)) * 2.0 ** -30
        if o[r] < 2:
            x[r, :, 0, :, 0] = rng.choice([-1.0, 1.0], (8, C))
            x[r, :, 11, :, 0] = 2.0 ** -10
        if o[r] == 2:
            for g in rng.permutation(8)[:4]: x[r, g, 0, rng.integers(C), 0] = 2.0 ** 29
        for h in range(0, 128, 16):
            u[r, h + 8, h] = k
            if o[r] < 2:
                u[r, h, h, 0] = k
                u[r, h + 11, h, 0] = k
            if o[r] == 2: u[r, h, h, 0] = 1.0
            if o[r] == 3 and h // 16 in low: u[r, h + 9, h] = -k
    still = [0, 8, 9, 10, 11, 12, 13, 14, 15]
    w = layers(rng, still)
    w[:, :, still] = 0
    return {"x": x.reshape(N, 128, 4 * C).astype(BF), "u": u.reshape(N, 128, 512), "v": d["v"], "p": lists(throws(rng, holes(rng))), **weights(rng, w)}
def setup_inputs_huge(rng):
    d = numbers_of(rng)
    h, o = rng.permutation(8), rng.permutation(N)
    c = rng.choice([-1.0, 1.0], (N, 1, 1, C, 1))
    c[o == 0] = 1.0
    x = (0.9 + 0.1 * rng.random((N, 8, 16, C, 4))) * 2.0 ** 30
    x[:, h[4:]] *= c
    a = (0.9 + 0.1 * rng.random((N, 8, 16, 8, 4))) * 2.0 ** 30
    for r in range(N):
        if o[r] == 0: a[r] *= -1.0
        elif o[r] % 2 == 1:
            a[r] *= -1.0
            a[r, h[4:]] = 0
        else: a[r, h[:4]] = 0
    u = d["u"].reshape(N, 128, 128, 4)
    u[:, :, ::16] = a.reshape(N, 128, 8, 4).astype(np.float32).astype(BF)
    w = np.zeros((N, 128, 4, 128, 4), np.float32)
    i = np.arange(128)
    for b in range(4): w[:, i, b, i, b] = -1
    return {"x": x.astype(np.float32).reshape(N, 128, 4 * C).astype(BF), "u": u.reshape(N, 128, 512), "v": d["v"], "p": lists(throws(rng, holes(rng))), **weights(rng, w.astype(BF))}
def setup_inputs_edges(rng):
    d = numbers_of(rng)
    h, a = rng.permutation(8), holes(rng)
    a[:, h[:2]] = np.arange(H)
    a[:, h[2:4]] = np.arange(C - 1 - H, C - 1)
    e = throws(rng, a)
    e[:, h[:2]] = np.arange(C) + H
    x = d["x"].reshape(N, 8, 16, C, 4)
    x[:, :, :3] = 0
    for r in range(N):
        for g in range(8):
            n = np.zeros(C, np.int64)
            n[meet(rng, e[r, g])] = np.arange(C - 1, -1, -1)
            for i in range(3): x[r, g, i, :, 0] = ((n >> (6 - 3 * i)) & 7).astype(np.float32).astype(BF)
    k = np.exp2(rng.integers(-2, 3, (N, 8, 1, C, 1)))
    b = (2 * rng.integers(0, 8, (N, 8, 8, C, 4)) + 1) * 2.0 ** -16 * k
    b[:, :, 0, :, 0] = 1.96875 * k[:, :, 0, :, 0]
    b *= rng.choice([-1.0, 1.0], b.shape)
    x[:, :, 8:] = b.astype(np.float32).astype(BF)
    u = d["u"].reshape(N, 128, 128, 4)
    u[:, :, ::16] = 0
    for g in range(0, 128, 16):
        for i in range(3): u[:, g + i, g, 0] = 2.0 ** (6 - 3 * i)
    return {"x": x.reshape(N, 128, 4 * C), "u": u.reshape(N, 128, 512), "v": d["v"], "p": lists(e), **weights(rng, layers(rng, [0, 1, 2, 8, 9, 10, 11, 12, 13, 14, 15]))}
def setup_inputs_spread(rng):
    d = setup_inputs(rng)
    d["x"] = big(wide(rng, N, 128, 4 * C, cols=6))
    return d
def check_inputs(d):
    b = []
    for k in ("x", "u", "v"):
        a = np.abs(d[k].astype(np.float32))
        if not (np.isfinite(a).all() and ((a == 0) | (a >= 2.0 ** -30) & (a <= 2.0 ** 30)).all()): b.append("a value of " + k)
    e = np.stack([gentries(d["p"][r]) for r in range(N)]).astype(np.int64)
    t, s = e - np.arange(C), np.sort(e, axis=2)
    if ((t < 0) | (t >= C)).any(): b.append("p: a landing out of its column's bounds")
    if (s[:, :, 1:] == s[:, :, :-1]).any(): b.append("p: equal landings")
    if (np.count_nonzero(e >= C, axis=2) != H).any(): b.append("p: the number of crossing landings")
    k = np.concatenate([s[:, :, :C - H], np.roll(s[:, :, C - H:], 1, axis=0) - C], axis=2)
    if (np.sort(k, axis=2) != np.arange(C)).any(): b.append("p: crossing landings aren't the next rank's holes")
    none, least, most = [emit(mx_ref.quantize(np.full((128, 16), k, np.float32).astype(BF)))[1][0, 0] for k in (0.0, 2.0 ** -30, 2.0 ** 30)]
    for r in range(N):
        if ((d["wc"][r] == 0x7F) | (d["wc"][r] == 0xFF)).any(): b.append("wc: a code that is no number")
        s = mx_ref.live(d["ws"][r])
        if ((s != none) & ((s < least) | (s > most))).any(): b.append("ws: a scale out of range")
    return b
def reference(x, u, v, p, wc, ws):
    qu = [mx_ref.quantize(u[r]) for r in range(N)]
    lay = [pk(wc[r], ws[r]) for r in range(N)]
    now = [x[r] for r in range(N)]
    land = np.stack([gentries(p[r]) for r in range(N)]).astype(np.int64)
    for t in range(R):
        for r in range(N):
            s = mx_ref.matmul(qu[r], mx_ref.quantize(now[r]))[::16] + np.float32(0.0)
            o = np.argsort(-s, axis=1, kind="stable")
            a, b = o[:, ::2], o[:, 1::2]
            la, lb = np.take_along_axis(land[r], a, axis=1), np.take_along_axis(land[r], b, axis=1)
            ok = (a <= lb) & (lb < a + C) & (b <= la) & (la < b + C)
            np.put_along_axis(land[r], a, np.where(ok, lb, la), axis=1)
            np.put_along_axis(land[r], b, np.where(ok, la, lb), axis=1)
        back, hits = np.argsort(land, axis=2), np.sort(land, axis=2)
        given = [mx_ref.quantize(gcols(now[r], back[r][:, C - H:])) for r in range(N)]
        new = []
        for r in range(N):
            both = np.concatenate([now[r], decode(given[r - 1]).astype(BF)], axis=1)
            e = np.zeros((8, C), np.int64)
            np.put_along_axis(e, hits[r][:, :C - H], back[r][:, :C - H], axis=1)
            np.put_along_axis(e, hits[r - 1][:, C - H:] - C, np.stack([C + np.arange(H)] * 8), axis=1)
            z = ((gcols(both, e).astype(np.float32) + now[r].astype(np.float32)) * np.float32(0.5)).astype(BF)
            q = mx_ref.quantize(z)
            new.append(tile([mx_ref.matmul(pick(lay[r], np.arange(128 * b, 128 * b + 128)), q) * np.float32(0.03125) + z[:, b::4].astype(np.float32) for b in range(4)]))
        now = new
    y, ol = np.zeros((N, 128, C), np.float32), np.zeros((N, 8, C), np.float32)
    oc, osc = np.zeros((N, 128, 4 * C), np.uint8), np.zeros((N, 16, C), np.uint8)
    for r in range(N):
        q = mx_ref.quantize(now[r])
        y[r] = mx_ref.matmul(mx_ref.quantize(v[r]), q)
        ol[r] = land[r]
        oc[r], osc[r] = emit(q)
    return {"y": y, "ol": ol, "oc": oc, "osc": osc}

@@ -1,0 +1,394 @@
+from concourse.bass import IndirectOffsetOnAxis
+from concourse.mybir import dt, AluOpType, ActivationFunctionType
+
+C = 384
+ROUNDS = 3
+BIG = 1e29
+HOLD = 1048576
+Q8 = "float8_e4m3fn_x4"
+A_ = AluOpType
+COPY = ActivationFunctionType.Copy
+INTS = "P24 T16 T1 TS k24 kb kc ic pi pm k1 k2 k3 k4 xi L I cx cc okk dl ok od Ln oi own y2".split()
+FLOATS = "rs RA KA wa rf fk".split()
+PARTS = {"rs": 24, "e2": 2, "cx": 2, "Ln": 2, "zt0": 4, "zt1": 4, "Ce": 2}
+for _i in range(6):
+    PARTS["C%d" % _i] = 4
+for _i in range(1, ROUNDS + 1):
+    PARTS["xt%da" % _i] = PARTS["xt%db" % _i] = 4
+
+
+def _ncols(a):
+    return max(128, 64 * (a + 1))
+
+
+SCRATCH = {"LI": ("sbuf", [128, 24 * len(INTS)], "int32"), "LF": ("sbuf", [128, 24 * len(FLOATS)], "float32")}
+
+
+def _sb(name, cols, dtype):
+    SCRATCH[name] = ("sbuf", [128, cols], dtype)
+
+
+for _i in range(ROUNDS + 1):
+    _sb("xt%d" % _i, 4 * C, "bfloat16")
+    _sb("qx%d" % _i, C, Q8)
+    _sb("sx%d" % _i, C, "uint8")
+    SCRATCH["wd%d" % _i] = ("dram", [8, C], "float32")
+for _i in range(ROUNDS):
+    _sb("land%d" % _i, C, Q8)
+    _sb("lans%d" % _i, C, "uint8")
+    _sb("sl%d" % _i, 24, "int32")
+    _sb("al%d" % _i, 24, "int32")
+for _i in range(4):
+    _sb("win%d" % _i, 896, "bfloat16")
+    _sb("eq%d" % _i, 128, Q8)
+    _sb("es%d" % _i, 128, "uint8")
+for _i in range(6):
+    _sb("C%d" % _i, 4 * _ncols(_i), "bfloat16")
+    _sb("cq%d" % _i, _ncols(_i), Q8)
+    _sb("cs%d" % _i, _ncols(_i), "uint8")
+for _n, _c, _d in (
+        ("Ce", 4 * C, "bfloat16"), ("ceq", C, Q8), ("ces", C, "uint8"),
+        ("ut", 512, "bfloat16"), ("uq", 128, Q8), ("us", 128, "uint8"), ("u16q", 128, Q8), ("u16s", 128, "uint8"),
+        ("vt", 512, "bfloat16"), ("vq", 128, Q8), ("vs", 128, "uint8"),
+        ("wq", 512, Q8), ("wsc", 512, "uint8"), ("xh", 4 * C, "bfloat16"), ("et", 520, "bfloat16"),
+        ("zt", 4 * C, "bfloat16"), ("zf", 4 * C, "bfloat16"), ("zq", C, Q8), ("zs", C, "uint8"),
+        ("gt0", 512, "bfloat16"), ("gt", 512, "bfloat16"), ("gq", 128, Q8), ("gs", 128, "uint8"),
+        ("zb", 768, "bfloat16"), ("ob", 520, "bfloat16"), ("junk", 24 * C, "bfloat16"),
+        ("D", C, "int32"), ("DA", C, "int32"), ("em", C, "float32"), ("mb", C, "float32"), ("d0", C, "float32"),
+        ("c2", C, "float32"), ("M", C, "float32"), ("h", C, "float32"), ("U8", 8, "int32"), ("idx", 2, "int32"),
+        ("pP", 24, "uint16"), ("pS", 24, "uint16"), ("upo", 8, "uint16"), ("e1", C, "float32"), ("ru", 24, "uint16"),
+        ("WT", C, "float32"), ("WB", C, "float32"), ("WN", C, "float32"), ("WS", C, "float32"),
+        ("e2", C, "float32"), ("Lu", 24, "uint16"), ("TLW", 768, "float32"), ("e3", C, "float32"),
+        ("e4", C, "float32"), ("tz", 24, "int32"), ("tl", 24, "uint16"), ("ysb", C, "float32")):
+    _sb(_n, _c, _d)
+for _i in range(8):
+    SCRATCH["P%d" % _i] = ("psum", [128, 512], "float32")
+SEMAPHORES = (["sV", "sA", "sT", "sG", "loc", "lx", "lp", "lu", "lv", "lw", "ls", "oy0", "oy1", "ool", "ooc"]
+              + ["oos%d" % k for k in range(4)] + ["dw%d" % k for k in range(4)] + ["ig%d" % k for k in range(4)]
+              + ["aq%d" % k for k in range(3)] + ["al%d" % k for k in range(3)])
+
+
+def rank_program(g, core, T, topo):
+    rank = T.rank_of(core)
+    if rank is None:
+        return
+    nxt = T.cores[(rank + 1) % len(T.cores)]
+    rid, pid = topo.addr(nxt)[:2]
+    mask = topo.mask(core, nxt)
+    neng = len(topo.engines(core, nxt))
+    prv = T.cores[(rank - 1) % len(T.cores)]
+    peng = len(topo.engines(prv, core))
+    V, AC, PE = g.vector, g.scalar, g.tensor
+    queue = {"V": V, "A": AC, "T": PE, "G": g, "S": g.sync}
+    own = {"V": "sV", "A": "sA", "T": "sT", "G": "sG"}
+    cnt, known = {}, {q: {} for q in queue}
+    wr, rd = {}, {}
+
+    def ex(keys):
+        return [p for k in keys for p in (["%s.%d" % (k, i) for i in range(PARTS[k])] if k in PARTS else [k])]
+
+    def before(q, R, W, adds=False):
+        toks = []
+        for k in ex(R):
+            if k in wr:
+                toks.append(wr[k])
+        for k in ex(W):
+            for t in ([wr[k]] if k in wr else []) + rd.get(k, []):
+                if adds and t[2] == q:
+                    continue
+                toks.append(t)
+        best = {}
+        for t in toks:
+            if known[q].get(t[0], 0) < t[1] and (t[0] not in best or best[t[0]][1] < t[1]):
+                best[t[0]] = t
+        keep = [t for t in best.values() if not any(o is not t and o[3].get(t[0], 0) >= t[1] for o in best.values())]
+        for t in keep:
+            queue[q].wait_ge(T.sem[t[0]], t[1])
+            for s, c in list(t[3].items()) + [(t[0], t[1])]:
+                known[q][s] = max(known[q].get(s, 0), c)
+
+    def after(q, sem, n, R, W):
+        cnt[sem] = cnt.get(sem, 0) + n
+        clk = dict(known[q])
+        clk[sem] = cnt[sem]
+        tok = (sem, cnt[sem], q, clk)
+        for k in ex(R):
+            rd[k] = [t for t in rd.get(k, []) if t[0] != sem] + [tok]
+        for k in ex(W):
+            wr[k] = tok
+            rd[k] = []
+
+    def op(q, R, W, f, adds=False):
+        before(q, R, W, adds)
+        f().then_inc(T.sem[own[q]], 1)
+        after(q, own[q], 1, R, W)
+
+    def dma(q, sem, R, W, f):
+        before(q, R, W)
+        f().then_inc(T.sem[sem], 16)
+        after(q, sem, 16, R, W)
+
+    def b8(v):
+        return v.bitcast(dt.uint8)
+
+    def li(name, lo=0, hi=24):
+        o = 24 * INTS.index(name)
+        return T.LI[:, o + lo:o + hi]
+
+    def lf(name, lo=0, hi=24):
+        o = 24 * FLOATS.index(name)
+        return T.LF[:, o + lo:o + hi]
+
+    def ts(R, W, out, in0, s1, s2, op0, op1=None):
+        if op1 is None:
+            op("V", R, W, lambda: V.tensor_scalar(out, in0, s1, None, op0))
+        else:
+            op("V", R, W, lambda: V.tensor_scalar(out, in0, s1, s2, op0, op1))
+
+    def tt(R, W, out, a, b, o):
+        op("V", R, W, lambda: V.tensor_tensor(out, a, b, o))
+
+    def cp(R, W, out, a):
+        op("V", R, W, lambda: V.tensor_copy(out, a))
+
+    def act(R, W, out, a, scale=None):
+        if scale is None:
+            op("A", R, W, lambda: AC.activation(out, a, COPY))
+        else:
+            op("A", R, W, lambda: AC.activation(out, a, COPY, scale=scale))
+
+    def quant(R, W, q, s, t):
+        op("V", R, W, lambda: V.quantize_mx(q, s, t))
+
+    def scan(R, W, out, d0, d1, init, o0, o1):
+        op("V", R, W, lambda: V.tensor_tensor_scan(out, d0, d1, init, o0, o1))
+
+    def mm(R, W, out, lq, ls_, rq, rs_, start=True, stop=True):
+        op("T", R, W, lambda: PE.matmul_mx(out, lq, ls_, rq, rs_, start, stop), not start)
+
+    def arrives(key, sem, n):
+        cnt[sem] = n
+        wr[key] = (sem, n, "-", {})
+
+    for t in range(ROUNDS):
+        arrives("land%d" % t, "aq%d" % t, 2 * peng)
+        arrives("al%d" % t, "al%d" % t, peng)
+
+    dma("S", "lx", [], ["xt0a", "xt0b"], lambda: g.sync.dma_start(T.xt0[:], T.x[:]))
+    dma("A", "lu", [], ["ut"], lambda: AC.dma_start(T.ut[:], T.u[:]))
+    dma("S", "lp", [], ["pi"], lambda: g.sync.dma_start(li("pi"), T.p[:]))
+
+    op("G", [], ["D"], lambda: g.iota(T.D[:], [[1, C]], 128, -1))
+    op("G", [], ["U8"], lambda: g.iota(T.U8[:], [[16, 8]], 0, 0))
+    op("G", [], ["P24"], lambda: g.iota(li("P24"), [[0, 24]], 0, 1))
+    op("G", [], ["T16"], lambda: g.iota(li("T16"), [[16, 24]], 0, 0))
+    op("G", [], ["T1"], lambda: g.iota(li("T1"), [[1, 24]], 0, 0))
+    op("G", [], ["TS"], lambda: g.iota(li("TS"), [[1, 12], [192, 2]], 0, 0))
+    op("V", [], ["zb"], lambda: V.memset(T.zb[:], 0.0))
+    op("V", [], ["ob"], lambda: V.memset(T.ob[:], 1.0))
+    op("V", [], ["rs"], lambda: V.memset(lf("rs"), 0.0))
+    op("G", ["ob"], ["gt0"], lambda: g.affine_select(T.gt0[:], T.ob[:, 0:512], [[-16, 8], [0, 64]], A_.is_ge, 0.0, 0, 1))
+    op("G", ["gt0"], ["gt"], lambda: g.affine_select(T.gt[:], T.gt0[:], [[16, 8], [0, 64]], A_.is_ge, 0.0, 15, -1))
+    op("G", ["ob"], ["et"], lambda: g.affine_select(T.et[:], T.ob[:], [[1, 520]], A_.is_equal, 0.0, -4, -4))
+    for a in range(6):
+        lo, hi = 256 * a, max(512, 256 * a + 256)
+        act(["zb"], ["C%d" % a], T["C%d" % a][:, lo:hi], T.zb[:, 0:hi - lo])
+    act(["zb"], ["Ce.0"], T.Ce[:, 0:768], T.zb[:])
+    act(["zb"], ["Ce.1"], T.Ce[:, 768:1536], T.zb[:])
+    for b in range(4):
+        act(["zb"], ["gap%d" % b], T["win%d" % b][:, 384:512], T.zb[:, 0:128])
+    ts(["D"], ["DA"], T.DA[:], T.D[:], 15, None, A_.bitwise_and)
+    cp(["U8"], ["upo"], T.upo[:], T.U8[:])
+    ts(["P24"], ["k24"], li("k24"), li("P24"), 15, None, A_.bitwise_and)
+    ts(["P24"], ["idx"], T.idx[:, 0:1], li("P24", 0, 1), 4, None, A_.logical_shift_right)
+    ts(["DA"], ["em"], T.em[:], T.DA[:], 0, None, A_.is_equal)
+    tt(["T16", "k24"], ["ic"], li("ic"), li("T16"), li("k24"), A_.add)
+    ts(["k24"], ["kb"], li("kb"), li("k24"), HOLD, None, A_.mult)
+    ts(["em"], ["d0"], T.d0[:], T.em[:], 2 * BIG, -BIG, A_.mult, A_.add)
+    ts(["em"], ["mb"], T.mb[:], T.em[:], -2 * BIG, BIG, A_.mult, A_.add)
+    op("V", [], ["d0"], lambda: V.memset(T.d0[:, 0:C:16], BIG))
+    quant(["ut"], ["uq"], T.uq[:, 0:128], T.us[:, 0:128], T.ut[:])
+    ts(["em"], ["c2"], T.c2[:], T.em[:], -1.0e8, float(HOLD), A_.mult, A_.add)
+    cp(["uq", "upo"], ["u16q"], T.u16q[:, 0:128].bitcast(dt.uint32),
+       T.uq[:, 0:128].bitcast(dt.uint32).indirect(T.upo[:, 0:8]))
+    act(["uq", "upo"], ["u16s"], T.u16s[:, 0:128], T.us[:, 0:128].indirect(T.upo[:, 0:8]))
+    ts(["ic"], ["pm"], li("pm"), li("ic"), 1024, 524288, A_.mult, A_.add)
+    ts(["k24"], ["k1"], li("k1"), li("k24"), 24, None, A_.mult)
+    tt(["pm", "pi"], ["wa"], lf("wa"), li("pm"), li("pi"), A_.add)
+    dma("S", "dw0", ["wa"], ["wd0"], lambda: g.sync.dma_start(T.wd0[:], lf("wa")))
+    tt(["kb", "T16"], ["kc"], li("kc"), li("T16"), li("kb"), A_.add)
+    tt(["k1", "T1"], ["k3"], li("k3"), li("k1"), li("T1"), A_.add)
+    ts(["k24"], ["k2"], li("k2"), li("k24"), 12, None, A_.mult)
+    ts(["kb"], ["fk"], lf("fk"), li("kb"), -1, 15 * HOLD + 511, A_.mult, A_.add)
+    ts(["kc"], ["KA"], lf("KA"), li("kc"), -1 - 15 * HOLD, None, A_.add)
+    cp(["k3"], ["pP"], T.pP[:], li("k3"))
+    tt(["k2", "TS"], ["k4"], li("k4"), li("k2"), li("TS"), A_.add)
+    cp(["k4"], ["pS"], T.pS[:], li("k4"))
+    dma("S", "lw", ["xt0a"], ["wq"], lambda: g.sync.dma_start(b8(T.wq[:, 0:512]), T.wc[:]))
+    dma("S", "ls", [], ["wsc"], lambda: g.sync.dma_start(T.wsc[:, 0:512], T.ws[:]))
+    dma("S", "lv", [], ["vt"], lambda: g.sync.dma_start(T.vt[:], T.v[:]))
+
+    def spread(i):
+        dma("G", "ig%d" % i, ["wd%d" % i, "idx"], ["WT"], lambda: g.indirect_dma_start(
+            T.WT[:], None, T["wd%d" % i][:], IndirectOffsetOnAxis(ap=T.idx[:, 0:1], axis=0), bounds_check=7))
+
+    spread(0)
+
+    for t in range(ROUNDS):
+        xt, qx, sx = T["xt%d" % t], T["qx%d" % t], T["sx%d" % t]
+        kx = ["xt%da" % t, "xt%db" % t]
+        kq = "qx%d" % t
+
+        def half(b):
+            act(kx, ["winx%d" % b], T["win%d" % b][:, 0:C], xt[:, b:4 * C:4], 2.0 ** -6)
+
+        quant(kx, [kq], qx[:, 0:C], sx[:, 0:C], xt[:])
+        mm(["u16q", "u16s", kq], ["P0"], T.P0[:, 0:C], T.u16q[:, 0:128], T.u16s[:, 0:128], qx[:, 0:C], sx[:, 0:C])
+        half(0)
+        half(1)
+        if t:
+            act(["WT", "pS"], ["WB"], T.WB[:], T.WT[:, 0:C].indirect(T.pS[:, 0:24]))
+            act(["WB", "ru"], ["WN"], T.WN[:], T.WB[:, 0:C].indirect(T.ru[:, 0:24]))
+        before("G", [kq], [])
+        g.remote_dma(b8(T["land%d" % t][:, 0:C]), b8(qx[:, 0:C]), T.sem["aq%d" % t], T.sem.loc, pid, rid, mask)
+        g.remote_dma(T["lans%d" % t][:, 0:C], sx[:, 0:C], T.sem["aq%d" % t], T.sem.loc, pid, rid, mask)
+        cnt["loc"] = cnt.get("loc", 0) + 2 * neng
+        if t == 0:
+            quant(["gt"], ["gq"], T.gq[:, 0:128], T.gs[:, 0:128], T.gt[:])
+            for b in range(4):
+                quant(["et"], ["eq%d" % b], T["eq%d" % b][:, 0:128], T["es%d" % b][:, 0:128], T.et[:, 4 - b:516 - b])
+        tt(["P0", "mb"], ["M"], T.M[:], T.P0[:, 0:C], T.mb[:], A_.max)
+        scan(["d0", "M"], ["h"], T.h[:], T.d0[:], T.M[:], BIG, A_.max, A_.min)
+
+        def compare(a):
+            Ct = T["C%d" % a]
+            for b in (3, 2, 1, 0):
+                w = 16 * (4 * a + b) + 16
+                ts(["P0", "h"], ["C%d.%d" % (a, b)], Ct[:, b:4 * w:4], T.P0[:, 0:w], T.h[:, w - 1:w], None, A_.is_lt)
+            for b in (3, 2, 1, 0):
+                j = 4 * a + b
+                if j:
+                    op("A", ["C%d.%d" % (a, b)], ["rs.%d" % j, "junk%d" % j], lambda: AC.activation(
+                        T.junk[:, C * j:C * j + 16 * j], Ct[:, b:64 * j:4], COPY, accum_out=lf("rs", j, j + 1)))
+
+        def count(a, start=False, stop=False):
+            n = _ncols(a)
+            quant(["C%d" % a], ["cq%d" % a], T["cq%d" % a][:, 0:n], T["cs%d" % a][:, 0:n], T["C%d" % a][:, 0:4 * n])
+            mm(["gq", "cq%d" % a], ["P1"], T.P1[:, 0:n], T.gq[:, 0:128], T.gs[:, 0:128],
+               T["cq%d" % a][:, 0:n], T["cs%d" % a][:, 0:n], start, stop)
+
+        compare(5)
+        compare(4)
+        count(5, start=True)
+        compare(3)
+        count(4)
+        tt(["h", "P0"], ["Ce"], T.Ce[:, 0:4 * C:4], T.h[:], T.P0[:, 0:C], A_.is_equal)
+        count(3)
+        compare(2)
+        quant(["Ce"], ["ceq"], T.ceq[:, 0:C], T.ces[:, 0:C], T.Ce[:])
+        mm(["gq", "ceq"], ["P1"], T.P1[:, 0:C], T.gq[:, 0:128], T.gs[:, 0:128], T.ceq[:, 0:C], T.ces[:, 0:C], False, False)
+        compare(1)
+        count(2)
+        compare(0)
+        count(1)
+        count(0, stop=True)
+        if t == 0:
+            act(["WT", "pP"], ["WN"], T.WN[:], T.WT[:, 0:C].indirect(T.pP[:, 0:24]))
+        act(["zb"], ["TLW"], T.TLW[:], T.zb[:])
+        half(2)
+        half(3)
+        act(kx, ["xh"], T.xh[:], xt[:], 2.0 ** -6)
+        for b in range(4):
+            mm(["eq%d" % b, "land%d" % t], ["P%d" % (2 + b)], T["P%d" % (2 + b)][:, 0:C], T["eq%d" % b][:, 0:128],
+               T["es%d" % b][:, 0:128], T["land%d" % t][:, 0:C], T["lans%d" % t][:, 0:C])
+        for b in range(4):
+            act(["P%d" % (2 + b)], ["wind%d" % b], T["win%d" % b][:, 512:896], T["P%d" % (2 + b)][:, 0:C], 2.0 ** -6)
+        tt(["KA", "rs"], ["RA"], lf("RA"), lf("KA"), lf("rs"), A_.subtract)
+        scan(["c2", "P1"], ["e1"], T.e1[:], T.c2[:], T.P1[:, 0:C], 0.0, A_.add, A_.max)
+        tt(["e1", "RA"], ["rf"], lf("rf"), T.e1[:, 15:C:16], lf("RA"), A_.add)
+        cp(["rf"], ["ru"], T.ru[:], lf("rf"))
+        cp(["ru", "WN"], ["WS"], T.WS[:, 0:C].indirect(T.ru[:, 0:24]), T.WN[:])
+        scan(["c2", "WS"], ["e2.0"], T.e2[:, 0:192], T.c2[:, 0:192], T.WS[:, 0:C:2], 0.0, A_.add, A_.max)
+        scan(["c2", "WS"], ["e2.1"], T.e2[:, 192:384], T.c2[:, 0:192], T.WS[:, 1:C:2], 0.0, A_.add, A_.max)
+        cp(["e2"], ["xi"], li("xi"), T.e2[:, 15:C:16])
+        ts(["xi"], ["L"], li("L"), li("xi"), 1023, None, A_.bitwise_and)
+        ts(["xi"], ["I"], li("I"), li("xi"), 10, 511, A_.logical_shift_right, A_.bitwise_and)
+        tt(["L", "I"], ["cx.0"], li("cx", 0, 12), li("L", 12, 24), li("I", 0, 12), A_.subtract)
+        tt(["L", "I"], ["cx.1"], li("cx", 12, 24), li("L", 0, 12), li("I", 12, 24), A_.subtract)
+        tt(["L"], ["dl"], li("dl", 0, 12), li("L", 12, 24), li("L", 0, 12), A_.subtract)
+        ts(["cx"], ["cc"], li("cc"), li("cx"), 0, 383, A_.max, A_.min)
+        tt(["cc", "cx"], ["okk"], li("okk"), li("cc"), li("cx"), A_.is_equal)
+        tt(["okk"], ["ok"], li("ok", 0, 12), li("okk", 0, 12), li("okk", 12, 24), A_.mult)
+        tt(["ok", "dl"], ["od"], li("od", 0, 12), li("ok", 0, 12), li("dl", 0, 12), A_.mult)
+        tt(["L", "od"], ["Ln.0"], li("Ln", 0, 12), li("L", 0, 12), li("od", 0, 12), A_.add)
+        tt(["L", "od"], ["Ln.1"], li("Ln", 12, 24), li("L", 12, 24), li("od", 0, 12), A_.subtract)
+        cp(["Ln"], ["Lu"], T.Lu[:], li("Ln"))
+        kw = "wd%d" % (t + 1)
+        if t == ROUNDS - 1:
+            cp(["Ln"], ["wa"], lf("wa"), li("Ln"))
+            dma("S", "dw%d" % (t + 1), ["wa"], [kw], lambda: g.sync.dma_start(T[kw][:], lf("wa")))
+        cp(["Lu", "WS"], ["TLW"], T.TLW[:, 0:768].indirect(T.Lu[:, 0:12]), T.WS[:, 0:C:2])
+        cp(["Lu", "WS"], ["TLW"], T.TLW[:, 0:768].indirect(T.Lu[:, 12:24]), T.WS[:, 1:C:2])
+        scan(["c2", "TLW"], ["e3"], T.e3[:], T.c2[:], T.TLW[:, 384:768], 0.0, A_.add, A_.max)
+        ksl = "sl%d" % t
+        ts(["e3", "fk"], [ksl], T[ksl][:], T.e3[:, 15:C:16], lf("fk", 0, 1), 2.0 ** -10, A_.subtract, A_.mult)
+        before("G", [ksl], [])
+        g.remote_dma(T["al%d" % t][:], T[ksl][:], T.sem["al%d" % t], T.sem.loc, pid, rid, mask)
+        cnt["loc"] += neng
+        scan(["c2", "TLW"], ["e4"], T.e4[:], T.c2[:], T.TLW[:, 0:384], 0.0, A_.add, A_.max)
+        if t < ROUNDS - 1:
+            ts(["xi"], ["y2"], li("y2"), li("xi"), 1023 * 1024, None, A_.bitwise_and)
+        cp(["e4"], ["oi"], li("oi"), T.e4[:, 15:C:16])
+        if t < ROUNDS - 1:
+            tt(["Ln", "y2"], ["wa"], lf("wa"), li("Ln"), li("y2"), A_.add)
+        ts(["oi"], ["own"], li("own"), li("oi"), 10, 511, A_.logical_shift_right, A_.bitwise_and)
+        if t < ROUNDS - 1:
+            dma("S", "dw%d" % (t + 1), ["wa"], [kw], lambda: g.sync.dma_start(T[kw][:], lf("wa")))
+        spread(t + 1)
+        if t == 0:
+            quant(["vt"], ["vq"], T.vq[:, 0:128], T.vs[:, 0:128], T.vt[:])
+        tt(["own", "al%d" % t], ["tz"], T.tz[:], li("own"), T["al%d" % t][:], A_.add)
+        cp(["tz"], ["tl"], T.tl[:], T.tz[:])
+        banks = [[2, 3, 4, 5], [6, 7, 0, 1]]
+        for c in range(2):
+            lo, hi = 192 * c, 192 * c + 192
+            for b in range(4):
+                win = T["win%d" % b]
+                tt(["winx%d" % b, "gap%d" % b, "wind%d" % b, "xh", "tl"], ["zt%d.%d" % (c, b)],
+                   T.zt[:, 4 * lo + b:4 * hi:4], win[:, 0:896].indirect(T.tl[:, 12 * c:12 * c + 12]),
+                   T.xh[:, 4 * lo + b:4 * hi:4], A_.add)
+            quant(["zt%d" % c], ["zq%d" % c], T.zq[:, lo:hi], T.zs[:, lo:hi], T.zt[:, 4 * lo:4 * hi])
+            act(["zt%d" % c], ["zf%d" % c], T.zf[:, 4 * lo:4 * hi], T.zt[:, 4 * lo:4 * hi], 32.0)
+            for b in range(4):
+                k = "P%d" % banks[c][b]
+                mm(["wq", "wsc", "zq%d" % c], [k], T[k][:, 0:192], T.wq[:, 128 * b:128 * b + 128],
+                   T.wsc[:, 128 * b:128 * b + 128], T.zq[:, lo:hi], T.zs[:, lo:hi])
+        for c in range(2):
+            lo, hi = 192 * c, 192 * c + 192
+            for b in range(4):
+                k = "P%d" % banks[c][b]
+                tt([k, "zf%d" % c], ["xt%d%s.%d" % (t + 1, "ab"[c], b)], T["xt%d" % (t + 1)][:, 4 * lo + b:4 * hi:4],
+                   T[k][:, 0:192], T.zf[:, 4 * lo + b:4 * hi:4], A_.add)
+
+    quant(["xt3a", "xt3b"], ["qx3"], T.qx3[:, 0:C], T.sx3[:, 0:C], T.xt3[:])
+    for c in range(2):
+        k = "P%d" % (2 + c)
+        mm(["vq", "qx3"], [k], T[k][:, 0:192], T.vq[:, 0:128], T.vs[:, 0:128],
+           T.qx3[:, 192 * c:192 * c + 192], T.sx3[:, 192 * c:192 * c + 192])
+    act(["WT", "pS"], ["WB"], T.WB[:], T.WT[:, 0:C].indirect(T.pS[:, 0:24]))
+    act(["WB", "ru"], ["WN"], T.WN[:], T.WB[:, 0:C].indirect(T.ru[:, 0:24]))
+    dma("A", "ool", ["WN"], [], lambda: AC.dma_start(T.ol[:], T.WN[0:128:16, :]))
+    dma("S", "ooc", ["qx3"], [], lambda: g.sync.dma_start(T.oc[:, 0:4 * C], b8(T.qx3[:, 0:C])))
+    cp(["P2"], ["ysb0"], T.ysb[:, 0:192], T.P2[:, 0:192])
+    cp(["P3"], ["ysb1"], T.ysb[:, 192:384], T.P3[:, 0:192])
+    for k in range(2):
+        dma("A", "oos%d" % k, ["qx3"], [], lambda: AC.dma_start(
+            T.osc[4 * k:4 * k + 4, 0:C], T.sx3[32 * k:32 * k + 4, 0:C]))
+    dma("S", "oy0", ["ysb0"], [], lambda: g.sync.dma_start(T.y[:, 0:192], T.ysb[:, 0:192]))
+    dma("A", "oy1", ["ysb1"], [], lambda: AC.dma_start(T.y[:, 192:384], T.ysb[:, 192:384]))
+    for k in range(2, 4):
+        dma("S", "oos%d" % k, ["qx3"], [], lambda: g.sync.dma_start(
+            T.osc[4 * k:4 * k + 4, 0:C], T.sx3[32 * k:32 * k + 4, 0:C]))
+    for s, c in cnt.items():
+        if not any(kn.get(s, 0) >= c for kn in known.values()):
+            g.wait_ge(T.sem[s], c)

@@ -3,16 +3,20 @@ from concourse.mybir import dt, AluOpType, ActivationFunctionType
 
 C = 384
 ROUNDS = 3
-BIG = 1e29
+BIG = 2.0 ** 96
 HOLD = 1048576
+DROP = 2 ** 27
+NA = 1
 Q8 = "float8_e4m3fn_x4"
 A_ = AluOpType
-COPY = ActivationFunctionType.Copy
-INTS = "P24 T16 T1 TS k24 kb kc ic pi pm k1 k2 k3 k4 xi L I cx cc okk dl ok od Ln oi own y2".split()
-FLOATS = "rs RA KA wa rf fk".split()
-PARTS = {"rs": 24, "e2": 2, "cx": 2, "Ln": 2, "zt0": 4, "zt1": 4, "Ce": 2}
+FN = ActivationFunctionType
+COPY = FN.Copy
+INTS = "P24 T16 T1 k24 kb kc ic pi pm k1 k3 xi xj L L2 I I2 cx cx2 r r2 oi own y2 rf b1 b2 b3 b4".split()
+FLOATS = "rs RA KA wa fk".split()
+PARTS = {"rs": 24, "e2": 2, "xi": 2, "X1": 2, "M": 2, "zt0": 4, "zt1": 4, "Ce": 3}
 for _i in range(6):
     PARTS["C%d" % _i] = 4
+PARTS["C5"] = 4 + NA
 for _i in range(1, ROUNDS + 1):
     PARTS["xt%da" % _i] = PARTS["xt%db" % _i] = 4
 
@@ -47,23 +51,25 @@ for _i in range(6):
     _sb("cq%d" % _i, _ncols(_i), Q8)
     _sb("cs%d" % _i, _ncols(_i), "uint8")
 for _n, _c, _d in (
-        ("Ce", 4 * C, "bfloat16"), ("ceq", C, Q8), ("ces", C, "uint8"),
+        ("Ce", 4 * C, "bfloat16"), ("ceq", C, Q8), ("ces", C, "uint8"), ("sg", NA * C, "bfloat16"),
         ("ut", 512, "bfloat16"), ("uq", 128, Q8), ("us", 128, "uint8"), ("u16q", 128, Q8), ("u16s", 128, "uint8"),
         ("vt", 512, "bfloat16"), ("vq", 128, Q8), ("vs", 128, "uint8"),
         ("wq", 512, Q8), ("wsc", 512, "uint8"), ("xh", 4 * C, "bfloat16"), ("et", 520, "bfloat16"),
         ("zt", 4 * C, "bfloat16"), ("zf", 4 * C, "bfloat16"), ("zq", C, Q8), ("zs", C, "uint8"),
         ("gt0", 512, "bfloat16"), ("gt", 512, "bfloat16"), ("gq", 128, Q8), ("gs", 128, "uint8"),
-        ("zb", 768, "bfloat16"), ("ob", 520, "bfloat16"), ("junk", 24 * C, "bfloat16"),
-        ("D", C, "int32"), ("DA", C, "int32"), ("em", C, "float32"), ("mb", C, "float32"), ("d0", C, "float32"),
+        ("zb", 520, "bfloat16"), ("junk", 24 * C, "bfloat16"),
+        ("D", C, "float32"), ("mb", C, "float32"), ("kf", 8, "float32"), ("d0", C, "float32"),
         ("c2", C, "float32"), ("M", C, "float32"), ("h", C, "float32"), ("U8", 8, "int32"), ("idx", 2, "int32"),
-        ("pP", 24, "uint16"), ("pS", 24, "uint16"), ("upo", 8, "uint16"), ("e1", C, "float32"), ("ru", 24, "uint16"),
-        ("WT", C, "float32"), ("WB", C, "float32"), ("WN", C, "float32"), ("WS", C, "float32"),
+        ("pP", 24, "uint16"), ("rp", 24, "uint16"), ("upo", 8, "uint16"), ("e1", C, "float32"), ("ru", 24, "uint16"),
+        ("WT", C, "float32"), ("WN", C, "float32"), ("WS", C, "float32"),
         ("e2", C, "float32"), ("Lu", 24, "uint16"), ("TLW", 768, "float32"), ("e3", C, "float32"),
-        ("e4", C, "float32"), ("tz", 24, "int32"), ("tl", 24, "uint16"), ("ysb", C, "float32")):
+        ("e4", C, "float32"), ("tz", 24, "int32"), ("S", C, "float32"),
+        ("X0", 48, "float32"), ("X1", 48, "float32"), ("so", 48, "float32"), ("tl", 24, "uint16"),
+        ("ysb", C, "float32")):
     _sb(_n, _c, _d)
 for _i in range(8):
     SCRATCH["P%d" % _i] = ("psum", [128, 512], "float32")
-SEMAPHORES = (["sV", "sA", "sT", "sG", "loc", "lx", "lp", "lu", "lv", "lw", "ls", "oy0", "oy1", "ool", "ooc"]
+SEMAPHORES = (["sV", "sA", "sT", "sG", "loc", "lx", "ly", "lp", "lu", "lv", "lw", "ls", "oy0", "oy1", "ool", "oc0", "oc1"]
               + ["oos%d" % k for k in range(4)] + ["dw%d" % k for k in range(4)] + ["ig%d" % k for k in range(4)]
               + ["aq%d" % k for k in range(3)] + ["al%d" % k for k in range(3)])
 
@@ -174,57 +180,51 @@ def rank_program(g, core, T, topo):
         arrives("land%d" % t, "aq%d" % t, 2 * peng)
         arrives("al%d" % t, "al%d" % t, peng)
 
-    dma("S", "lx", [], ["xt0a", "xt0b"], lambda: g.sync.dma_start(T.xt0[:], T.x[:]))
+    dma("S", "lx", [], ["xt0a"], lambda: g.sync.dma_start(T.xt0[:, 0:768], T.x[:, 0:768]))
     dma("A", "lu", [], ["ut"], lambda: AC.dma_start(T.ut[:], T.u[:]))
+    dma("A", "ly", [], ["xt0b"], lambda: AC.dma_start(T.xt0[:, 768:1536], T.x[:, 768:1536]))
     dma("S", "lp", [], ["pi"], lambda: g.sync.dma_start(li("pi"), T.p[:]))
 
-    op("G", [], ["D"], lambda: g.iota(T.D[:], [[1, C]], 128, -1))
-    op("G", [], ["U8"], lambda: g.iota(T.U8[:], [[16, 8]], 0, 0))
     op("G", [], ["P24"], lambda: g.iota(li("P24"), [[0, 24]], 0, 1))
+    op("G", [], ["D"], lambda: g.iota(T.D[:], [[0, 24], [1, 16]], 0, 0, allow_small_or_imprecise_dtypes=True))
+    op("G", [], ["U8"], lambda: g.iota(T.U8[:], [[16, 8]], 0, 0))
     op("G", [], ["T16"], lambda: g.iota(li("T16"), [[16, 24]], 0, 0))
     op("G", [], ["T1"], lambda: g.iota(li("T1"), [[1, 24]], 0, 0))
-    op("G", [], ["TS"], lambda: g.iota(li("TS"), [[1, 12], [192, 2]], 0, 0))
     op("V", [], ["zb"], lambda: V.memset(T.zb[:], 0.0))
-    op("V", [], ["ob"], lambda: V.memset(T.ob[:], 1.0))
     op("V", [], ["rs"], lambda: V.memset(lf("rs"), 0.0))
-    op("G", ["ob"], ["gt0"], lambda: g.affine_select(T.gt0[:], T.ob[:, 0:512], [[-16, 8], [0, 64]], A_.is_ge, 0.0, 0, 1))
+    op("V", [], ["X0"], lambda: V.memset(T.X0[:], 0.0))
+    ts(["P24"], ["k24"], li("k24"), li("P24"), 15, None, A_.bitwise_and)
+    ts(["P24"], ["idx"], T.idx[:, 0:1], li("P24", 0, 1), 4, None, A_.logical_shift_right)
+    cp(["k24"], ["kf"], T.kf[:, 0:1], li("k24", 0, 1))
+    op("G", ["zb"], ["et"], lambda: g.affine_select(T.et[:], T.zb[:, 0:520], [[1, 520]], A_.not_equal, 1.0, -4, -4))
+    op("G", ["zb"], ["gt0"], lambda: g.affine_select(
+        T.gt0[:], T.zb[:, 0:512], [[16, 8], [0, 64]], A_.is_gt, 1.0, 0, -1))
     op("G", ["gt0"], ["gt"], lambda: g.affine_select(T.gt[:], T.gt0[:], [[16, 8], [0, 64]], A_.is_ge, 0.0, 15, -1))
-    op("G", ["ob"], ["et"], lambda: g.affine_select(T.et[:], T.ob[:], [[1, 520]], A_.is_equal, 0.0, -4, -4))
     for a in range(6):
         lo, hi = 256 * a, max(512, 256 * a + 256)
         act(["zb"], ["C%d" % a], T["C%d" % a][:, lo:hi], T.zb[:, 0:hi - lo])
-    act(["zb"], ["Ce.0"], T.Ce[:, 0:768], T.zb[:])
-    act(["zb"], ["Ce.1"], T.Ce[:, 768:1536], T.zb[:])
-    for b in range(4):
-        act(["zb"], ["gap%d" % b], T["win%d" % b][:, 384:512], T.zb[:, 0:128])
-    ts(["D"], ["DA"], T.DA[:], T.D[:], 15, None, A_.bitwise_and)
+    act(["zb"], ["Ce.0"], T.Ce[:, 0:512], T.zb[:, 0:512])
+    ts(["D", "kf"], ["mb"], T.mb[:], T.D[:], T.kf[:, 0:1], BIG, A_.not_equal, A_.mult)
+    ts(["D", "kf"], ["d0"], T.d0[:], T.D[:], T.kf[:, 0:1], BIG, A_.is_equal, A_.mult)
     cp(["U8"], ["upo"], T.upo[:], T.U8[:])
-    ts(["P24"], ["k24"], li("k24"), li("P24"), 15, None, A_.bitwise_and)
-    ts(["P24"], ["idx"], T.idx[:, 0:1], li("P24", 0, 1), 4, None, A_.logical_shift_right)
-    ts(["DA"], ["em"], T.em[:], T.DA[:], 0, None, A_.is_equal)
     tt(["T16", "k24"], ["ic"], li("ic"), li("T16"), li("k24"), A_.add)
-    ts(["k24"], ["kb"], li("kb"), li("k24"), HOLD, None, A_.mult)
-    ts(["em"], ["d0"], T.d0[:], T.em[:], 2 * BIG, -BIG, A_.mult, A_.add)
-    ts(["em"], ["mb"], T.mb[:], T.em[:], -2 * BIG, BIG, A_.mult, A_.add)
     op("V", [], ["d0"], lambda: V.memset(T.d0[:, 0:C:16], BIG))
-    quant(["ut"], ["uq"], T.uq[:, 0:128], T.us[:, 0:128], T.ut[:])
-    ts(["em"], ["c2"], T.c2[:], T.em[:], -1.0e8, float(HOLD), A_.mult, A_.add)
-    cp(["uq", "upo"], ["u16q"], T.u16q[:, 0:128].bitcast(dt.uint32),
-       T.uq[:, 0:128].bitcast(dt.uint32).indirect(T.upo[:, 0:8]))
-    act(["uq", "upo"], ["u16s"], T.u16s[:, 0:128], T.us[:, 0:128].indirect(T.upo[:, 0:8]))
+    ts(["k24"], ["kb"], li("kb"), li("k24"), HOLD, None, A_.mult)
     ts(["ic"], ["pm"], li("pm"), li("ic"), 1024, 524288, A_.mult, A_.add)
     ts(["k24"], ["k1"], li("k1"), li("k24"), 24, None, A_.mult)
     tt(["pm", "pi"], ["wa"], lf("wa"), li("pm"), li("pi"), A_.add)
     dma("S", "dw0", ["wa"], ["wd0"], lambda: g.sync.dma_start(T.wd0[:], lf("wa")))
     tt(["kb", "T16"], ["kc"], li("kc"), li("T16"), li("kb"), A_.add)
     tt(["k1", "T1"], ["k3"], li("k3"), li("k1"), li("T1"), A_.add)
-    ts(["k24"], ["k2"], li("k2"), li("k24"), 12, None, A_.mult)
     ts(["kb"], ["fk"], lf("fk"), li("kb"), -1, 15 * HOLD + 511, A_.mult, A_.add)
     ts(["kc"], ["KA"], lf("KA"), li("kc"), -1 - 15 * HOLD, None, A_.add)
     cp(["k3"], ["pP"], T.pP[:], li("k3"))
-    tt(["k2", "TS"], ["k4"], li("k4"), li("k2"), li("TS"), A_.add)
-    cp(["k4"], ["pS"], T.pS[:], li("k4"))
-    dma("S", "lw", ["xt0a"], ["wq"], lambda: g.sync.dma_start(b8(T.wq[:, 0:512]), T.wc[:]))
+    ts(["mb"], ["c2"], T.c2[:], T.mb[:], (DROP + HOLD) / BIG, -float(DROP), A_.mult, A_.add)
+    quant(["ut"], ["uq"], T.uq[:, 0:128], T.us[:, 0:128], T.ut[:])
+    cp(["uq", "upo"], ["u16q"], T.u16q[:, 0:128].bitcast(dt.uint32),
+       T.uq[:, 0:128].bitcast(dt.uint32).indirect(T.upo[:, 0:8]))
+    act(["uq", "upo"], ["u16s"], T.u16s[:, 0:128], T.us[:, 0:128].indirect(T.upo[:, 0:8]))
+    dma("S", "lw", ["xt0a", "xt0b"], ["wq"], lambda: g.sync.dma_start(b8(T.wq[:, 0:512]), T.wc[:]))
     dma("S", "ls", [], ["wsc"], lambda: g.sync.dma_start(T.wsc[:, 0:512], T.ws[:]))
     dma("S", "lv", [], ["vt"], lambda: g.sync.dma_start(T.vt[:], T.v[:]))
 
@@ -234,6 +234,22 @@ def rank_program(g, core, T, topo):
 
     spread(0)
 
+    def scores(t, c):
+        qx, sx, k = T["qx%d" % t], T["sx%d" % t], "P%d" % (2 + c)
+        lo, hi = 192 * c, 192 * c + 192
+        kq = "qx%d%s" % (t, "ab"[c])
+        quant(["xt%d%s" % (t, "ab"[c])], [kq], qx[:, lo:hi], sx[:, lo:hi], T["xt%d" % t][:, 4 * lo:4 * hi])
+        if t < ROUNDS:
+            mm(["u16q", "u16s", kq], [k], T[k][:, 0:192], T.u16q[:, 0:128], T.u16s[:, 0:128], qx[:, lo:hi], sx[:, lo:hi])
+            if c == 0:
+                if t == 0:
+                    act(["zb"], ["Ce.1"], T.Ce[:, 512:1024], T.zb[:, 0:512])
+                act([k], ["S0", "turn0"], T.S[:, 0:192], T[k][:, 0:192])
+                if t == 0:
+                    act(["zb"], ["Ce.2"], T.Ce[:, 1024:1536], T.zb[:, 0:512])
+        else:
+            mm(["vq", kq], [k], T[k][:, 0:192], T.vq[:, 0:128], T.vs[:, 0:128], qx[:, lo:hi], sx[:, lo:hi])
+
     for t in range(ROUNDS):
         xt, qx, sx = T["xt%d" % t], T["qx%d" % t], T["sx%d" % t]
         kx = ["xt%da" % t, "xt%db" % t]
@@ -242,30 +258,38 @@ def rank_program(g, core, T, topo):
         def half(b):
             act(kx, ["winx%d" % b], T["win%d" % b][:, 0:C], xt[:, b:4 * C:4], 2.0 ** -6)
 
-        quant(kx, [kq], qx[:, 0:C], sx[:, 0:C], xt[:])
-        mm(["u16q", "u16s", kq], ["P0"], T.P0[:, 0:C], T.u16q[:, 0:128], T.u16s[:, 0:128], qx[:, 0:C], sx[:, 0:C])
-        half(0)
-        half(1)
-        if t:
-            act(["WT", "pS"], ["WB"], T.WB[:], T.WT[:, 0:C].indirect(T.pS[:, 0:24]))
-            act(["WB", "ru"], ["WN"], T.WN[:], T.WB[:, 0:C].indirect(T.ru[:, 0:24]))
-        before("G", [kq], [])
+        if t == 0:
+            scores(0, 0)
+            scores(0, 1)
+        before("G", [kq + "a", kq + "b"], [])
         g.remote_dma(b8(T["land%d" % t][:, 0:C]), b8(qx[:, 0:C]), T.sem["aq%d" % t], T.sem.loc, pid, rid, mask)
         g.remote_dma(T["lans%d" % t][:, 0:C], sx[:, 0:C], T.sem["aq%d" % t], T.sem.loc, pid, rid, mask)
         cnt["loc"] = cnt.get("loc", 0) + 2 * neng
         if t == 0:
-            quant(["gt"], ["gq"], T.gq[:, 0:128], T.gs[:, 0:128], T.gt[:])
             for b in range(4):
                 quant(["et"], ["eq%d" % b], T["eq%d" % b][:, 0:128], T["es%d" % b][:, 0:128], T.et[:, 4 - b:516 - b])
-        tt(["P0", "mb"], ["M"], T.M[:], T.P0[:, 0:C], T.mb[:], A_.max)
-        scan(["d0", "M"], ["h"], T.h[:], T.d0[:], T.M[:], BIG, A_.max, A_.min)
+        tt(["P2", "mb", "turn0"], ["M.0"], T.M[:, 0:192], T.P2[:, 0:192], T.mb[:, 0:192], A_.add)
+        tt(["P3", "mb"], ["M.1", "turn1"], T.M[:, 192:384], T.P3[:, 0:192], T.mb[:, 192:384], A_.add)
+        act(["P3", "turn1"], ["S1"], T.S[:, 192:384], T.P3[:, 0:192])
+        scan(["d0", "M"], ["h"], T.h[:], T.d0[:], T.M[:], BIG, A_.add, A_.min)
+
+        for n in range(NA):
+            b = 3 - n
+            w = 16 * (20 + b)
+            op("A", ["S0", "S1", "h"], ["sg%d" % n], lambda: AC.activation(
+                T.sg[:, C * n:C * n + w], T.S[:, 0:w], FN.Sign, bias=T.h[:, w + 15:w + 16], scale=-1.0))
+            op("A", ["sg%d" % n], ["C5.%d" % (4 + n), "rs.%d" % (20 + b)], lambda: AC.activation(
+                T.C5[:, b:4 * w:4], T.sg[:, C * n:C * n + w], FN.Relu, accum_out=lf("rs", 20 + b, 21 + b)))
 
         def compare(a):
             Ct = T["C%d" % a]
-            for b in (3, 2, 1, 0):
+            mine = [b for b in (3, 2, 1, 0) if a < 5 or b < 4 - NA]
+            for b in mine + [b for b in (3, 2, 1, 0) if b not in mine]:
                 w = 16 * (4 * a + b) + 16
-                ts(["P0", "h"], ["C%d.%d" % (a, b)], Ct[:, b:4 * w:4], T.P0[:, 0:w], T.h[:, w - 1:w], None, A_.is_lt)
-            for b in (3, 2, 1, 0):
+                lo = 0 if b in mine else w - 16
+                ts(["S0", "S1", "h"], ["C%d.%d" % (a, b)], Ct[:, 4 * lo + b:4 * w:4], T.S[:, lo:w], T.h[:, w - 1:w], None,
+                   A_.is_lt)
+            for b in mine:
                 j = 4 * a + b
                 if j:
                     op("A", ["C%d.%d" % (a, b)], ["rs.%d" % j, "junk%d" % j], lambda: AC.activation(
@@ -278,117 +302,131 @@ def rank_program(g, core, T, topo):
                T["cq%d" % a][:, 0:n], T["cs%d" % a][:, 0:n], start, stop)
 
         compare(5)
+        if t == 0:
+            quant(["gt"], ["gq"], T.gq[:, 0:128], T.gs[:, 0:128], T.gt[:])
         compare(4)
         count(5, start=True)
         compare(3)
         count(4)
-        tt(["h", "P0"], ["Ce"], T.Ce[:, 0:4 * C:4], T.h[:], T.P0[:, 0:C], A_.is_equal)
+        for c in range(2):
+            lo, hi = 192 * c, 192 * c + 192
+            tt(["h", "P%d" % (2 + c), "S%d" % c], ["Ce.%d" % (2 * c), "eqs%d" % c] + (["Ce.1"] if c == 0 else []),
+               T.Ce[:, 4 * lo:4 * hi:4], T.h[:, lo:hi], T["P%d" % (2 + c)][:, 0:192], A_.is_equal)
         count(3)
         compare(2)
-        quant(["Ce"], ["ceq"], T.ceq[:, 0:C], T.ces[:, 0:C], T.Ce[:])
+        quant(["Ce", "eqs0", "eqs1"], ["ceq"], T.ceq[:, 0:C], T.ces[:, 0:C], T.Ce[:])
         mm(["gq", "ceq"], ["P1"], T.P1[:, 0:C], T.gq[:, 0:128], T.gs[:, 0:128], T.ceq[:, 0:C], T.ces[:, 0:C], False, False)
         compare(1)
         count(2)
         compare(0)
         count(1)
         count(0, stop=True)
-        if t == 0:
-            act(["WT", "pP"], ["WN"], T.WN[:], T.WT[:, 0:C].indirect(T.pP[:, 0:24]))
-        act(["zb"], ["TLW"], T.TLW[:], T.zb[:])
-        half(2)
-        half(3)
+        k = "rp" if t else "pP"
+        act(["WT", k], ["WN"], T.WN[:], T.WT[:, 0:C].indirect(T[k][:, 0:24]))
+        for c in range(2):
+            act(["zb"], ["TLW"] if c else ["TLWa"], T.TLW[:, 384 * c:384 * c + 384], T.zb[:, 0:384])
+        for b in range(4):
+            half(b)
+            if t == 0:
+                act(["zb"], ["gap%d" % b], T["win%d" % b][:, 384:512], T.zb[:, 0:128])
         act(kx, ["xh"], T.xh[:], xt[:], 2.0 ** -6)
         for b in range(4):
-            mm(["eq%d" % b, "land%d" % t], ["P%d" % (2 + b)], T["P%d" % (2 + b)][:, 0:C], T["eq%d" % b][:, 0:128],
+            mm(["eq%d" % b, "land%d" % t], ["P%d" % (4 + b)], T["P%d" % (4 + b)][:, 0:C], T["eq%d" % b][:, 0:128],
                T["es%d" % b][:, 0:128], T["land%d" % t][:, 0:C], T["lans%d" % t][:, 0:C])
         for b in range(4):
-            act(["P%d" % (2 + b)], ["wind%d" % b], T["win%d" % b][:, 512:896], T["P%d" % (2 + b)][:, 0:C], 2.0 ** -6)
+            act(["P%d" % (4 + b)], ["wind%d" % b], T["win%d" % b][:, 512:896], T["P%d" % (4 + b)][:, 0:C], 2.0 ** -6)
         tt(["KA", "rs"], ["RA"], lf("RA"), lf("KA"), lf("rs"), A_.subtract)
         scan(["c2", "P1"], ["e1"], T.e1[:], T.c2[:], T.P1[:, 0:C], 0.0, A_.add, A_.max)
-        tt(["e1", "RA"], ["rf"], lf("rf"), T.e1[:, 15:C:16], lf("RA"), A_.add)
-        cp(["rf"], ["ru"], T.ru[:], lf("rf"))
+        tt(["e1", "RA"], ["rf"], li("rf"), T.e1[:, 15:C:16], lf("RA"), A_.add)
+        cp(["rf"], ["ru"], T.ru[:], li("rf"))
         cp(["ru", "WN"], ["WS"], T.WS[:, 0:C].indirect(T.ru[:, 0:24]), T.WN[:])
         scan(["c2", "WS"], ["e2.0"], T.e2[:, 0:192], T.c2[:, 0:192], T.WS[:, 0:C:2], 0.0, A_.add, A_.max)
         scan(["c2", "WS"], ["e2.1"], T.e2[:, 192:384], T.c2[:, 0:192], T.WS[:, 1:C:2], 0.0, A_.add, A_.max)
-        cp(["e2"], ["xi"], li("xi"), T.e2[:, 15:C:16])
-        ts(["xi"], ["L"], li("L"), li("xi"), 1023, None, A_.bitwise_and)
-        ts(["xi"], ["I"], li("I"), li("xi"), 10, 511, A_.logical_shift_right, A_.bitwise_and)
-        tt(["L", "I"], ["cx.0"], li("cx", 0, 12), li("L", 12, 24), li("I", 0, 12), A_.subtract)
-        tt(["L", "I"], ["cx.1"], li("cx", 12, 24), li("L", 0, 12), li("I", 12, 24), A_.subtract)
-        tt(["L"], ["dl"], li("dl", 0, 12), li("L", 12, 24), li("L", 0, 12), A_.subtract)
-        ts(["cx"], ["cc"], li("cc"), li("cx"), 0, 383, A_.max, A_.min)
-        tt(["cc", "cx"], ["okk"], li("okk"), li("cc"), li("cx"), A_.is_equal)
-        tt(["okk"], ["ok"], li("ok", 0, 12), li("okk", 0, 12), li("okk", 12, 24), A_.mult)
-        tt(["ok", "dl"], ["od"], li("od", 0, 12), li("ok", 0, 12), li("dl", 0, 12), A_.mult)
-        tt(["L", "od"], ["Ln.0"], li("Ln", 0, 12), li("L", 0, 12), li("od", 0, 12), A_.add)
-        tt(["L", "od"], ["Ln.1"], li("Ln", 12, 24), li("L", 12, 24), li("od", 0, 12), A_.subtract)
-        cp(["Ln"], ["Lu"], T.Lu[:], li("Ln"))
+        cp(["e2"], ["xi.0"], li("xi"), T.e2[:, 15:C:16])
+        cp(["e2"], ["xi.1"], li("xj"), T.e2[:, 15:C:16])
+        ts(["xi"], ["L"], li("L", 0, 48), li("xi", 0, 48), 1023, None, A_.bitwise_and)
+        ts(["xi"], ["I"], li("I", 0, 36), li("xi", 0, 36), 10, 511, A_.logical_shift_right, A_.bitwise_and)
+        tt(["L", "I"], ["cx"], li("cx", 0, 36), li("L", 12, 48), li("I", 0, 36), A_.subtract)
+        tt(["L"], ["X1.0"], T.X1[:, 0:48:2], li("L", 12, 36), li("L", 0, 24), A_.subtract)
+        ts(["cx"], ["r"], li("r", 0, 36), li("cx", 0, 36), -191.5, 1.0 / 384, A_.add, A_.mult)
+        cp(["L"], ["X1.1"], T.X1[:, 1:48:2], li("L"))
+        tt(["r"], ["X0"], T.X0[:, 1:48:2], li("r", 0, 24), li("r", 12, 36), A_.is_equal)
+        scan(["X0", "X1"], ["so"], T.so[:], T.X0[:], T.X1[:], 0.0, A_.mult, A_.add)
+        cp(["so"], ["Lu"], T.Lu[:], T.so[:, 1:48:2])
         kw = "wd%d" % (t + 1)
         if t == ROUNDS - 1:
-            cp(["Ln"], ["wa"], lf("wa"), li("Ln"))
+            cp(["so"], ["wa"], lf("wa"), T.so[:, 1:48:2])
             dma("S", "dw%d" % (t + 1), ["wa"], [kw], lambda: g.sync.dma_start(T[kw][:], lf("wa")))
-        cp(["Lu", "WS"], ["TLW"], T.TLW[:, 0:768].indirect(T.Lu[:, 0:12]), T.WS[:, 0:C:2])
-        cp(["Lu", "WS"], ["TLW"], T.TLW[:, 0:768].indirect(T.Lu[:, 12:24]), T.WS[:, 1:C:2])
+        cp(["Lu", "WS"], ["TLW", "TLWa"], T.TLW[:, 0:768].indirect(T.Lu[:, 0:12]), T.WS[:, 0:C:2])
+        cp(["Lu", "WS"], ["TLW", "TLWa"], T.TLW[:, 0:768].indirect(T.Lu[:, 12:24]), T.WS[:, 1:C:2])
         scan(["c2", "TLW"], ["e3"], T.e3[:], T.c2[:], T.TLW[:, 384:768], 0.0, A_.add, A_.max)
         ksl = "sl%d" % t
         ts(["e3", "fk"], [ksl], T[ksl][:], T.e3[:, 15:C:16], lf("fk", 0, 1), 2.0 ** -10, A_.subtract, A_.mult)
         before("G", [ksl], [])
         g.remote_dma(T["al%d" % t][:], T[ksl][:], T.sem["al%d" % t], T.sem.loc, pid, rid, mask)
         cnt["loc"] += neng
-        scan(["c2", "TLW"], ["e4"], T.e4[:], T.c2[:], T.TLW[:, 0:384], 0.0, A_.add, A_.max)
+        scan(["c2", "TLW", "TLWa"], ["e4"], T.e4[:], T.c2[:], T.TLW[:, 0:384], 0.0, A_.add, A_.max)
         if t < ROUNDS - 1:
             ts(["xi"], ["y2"], li("y2"), li("xi"), 1023 * 1024, None, A_.bitwise_and)
         cp(["e4"], ["oi"], li("oi"), T.e4[:, 15:C:16])
         if t < ROUNDS - 1:
-            tt(["Ln", "y2"], ["wa"], lf("wa"), li("Ln"), li("y2"), A_.add)
+            tt(["so", "y2"], ["wa"], lf("wa"), T.so[:, 1:48:2], li("y2"), A_.add)
         ts(["oi"], ["own"], li("own"), li("oi"), 10, 511, A_.logical_shift_right, A_.bitwise_and)
         if t < ROUNDS - 1:
             dma("S", "dw%d" % (t + 1), ["wa"], [kw], lambda: g.sync.dma_start(T[kw][:], lf("wa")))
         spread(t + 1)
+        ts(["rf"], ["b1"], li("b1"), li("rf"), 31, None, A_.bitwise_and)
+        ts(["rf"], ["b2"], li("b2"), li("rf"), 5, None, A_.logical_shift_right)
+        ts(["b1"], ["b3"], li("b3"), li("b1"), 12, None, A_.mult)
+        tt(["b3", "b2"], ["b4"], li("b4"), li("b3"), li("b2"), A_.add)
+        cp(["b4"], ["rp"], T.rp[:], li("b4"))
         if t == 0:
             quant(["vt"], ["vq"], T.vq[:, 0:128], T.vs[:, 0:128], T.vt[:])
         tt(["own", "al%d" % t], ["tz"], T.tz[:], li("own"), T["al%d" % t][:], A_.add)
         cp(["tz"], ["tl"], T.tl[:], T.tz[:])
         banks = [[2, 3, 4, 5], [6, 7, 0, 1]]
-        for c in range(2):
+
+        def catch(c, b):
             lo, hi = 192 * c, 192 * c + 192
-            for b in range(4):
-                win = T["win%d" % b]
-                tt(["winx%d" % b, "gap%d" % b, "wind%d" % b, "xh", "tl"], ["zt%d.%d" % (c, b)],
-                   T.zt[:, 4 * lo + b:4 * hi:4], win[:, 0:896].indirect(T.tl[:, 12 * c:12 * c + 12]),
-                   T.xh[:, 4 * lo + b:4 * hi:4], A_.add)
+            tt(["winx%d" % b, "gap%d" % b, "wind%d" % b, "xh", "tl"], ["zt%d.%d" % (c, b)],
+               T.zt[:, 4 * lo + b:4 * hi:4], T["win%d" % b][:, 0:896].indirect(T.tl[:, 12 * c:12 * c + 12]),
+               T.xh[:, 4 * lo + b:4 * hi:4], A_.add)
+
+        def layer(c):
+            lo, hi = 192 * c, 192 * c + 192
             quant(["zt%d" % c], ["zq%d" % c], T.zq[:, lo:hi], T.zs[:, lo:hi], T.zt[:, 4 * lo:4 * hi])
             act(["zt%d" % c], ["zf%d" % c], T.zf[:, 4 * lo:4 * hi], T.zt[:, 4 * lo:4 * hi], 32.0)
             for b in range(4):
                 k = "P%d" % banks[c][b]
                 mm(["wq", "wsc", "zq%d" % c], [k], T[k][:, 0:192], T.wq[:, 128 * b:128 * b + 128],
                    T.wsc[:, 128 * b:128 * b + 128], T.zq[:, lo:hi], T.zs[:, lo:hi])
-        for c in range(2):
-            lo, hi = 192 * c, 192 * c + 192
-            for b in range(4):
-                k = "P%d" % banks[c][b]
-                tt([k, "zf%d" % c], ["xt%d%s.%d" % (t + 1, "ab"[c], b)], T["xt%d" % (t + 1)][:, 4 * lo + b:4 * hi:4],
-                   T[k][:, 0:192], T.zf[:, 4 * lo + b:4 * hi:4], A_.add)
 
-    quant(["xt3a", "xt3b"], ["qx3"], T.qx3[:, 0:C], T.sx3[:, 0:C], T.xt3[:])
-    for c in range(2):
-        k = "P%d" % (2 + c)
-        mm(["vq", "qx3"], [k], T[k][:, 0:192], T.vq[:, 0:128], T.vs[:, 0:128],
-           T.qx3[:, 192 * c:192 * c + 192], T.sx3[:, 192 * c:192 * c + 192])
-    act(["WT", "pS"], ["WB"], T.WB[:], T.WT[:, 0:C].indirect(T.pS[:, 0:24]))
-    act(["WB", "ru"], ["WN"], T.WN[:], T.WB[:, 0:C].indirect(T.ru[:, 0:24]))
-    dma("A", "ool", ["WN"], [], lambda: AC.dma_start(T.ol[:], T.WN[0:128:16, :]))
-    dma("S", "ooc", ["qx3"], [], lambda: g.sync.dma_start(T.oc[:, 0:4 * C], b8(T.qx3[:, 0:C])))
-    cp(["P2"], ["ysb0"], T.ysb[:, 0:192], T.P2[:, 0:192])
+        def state(c, b):
+            lo, hi = 192 * c, 192 * c + 192
+            k = "P%d" % banks[c][b]
+            tt([k, "zf%d" % c], ["xt%d%s.%d" % (t + 1, "ab"[c], b)], T["xt%d" % (t + 1)][:, 4 * lo + b:4 * hi:4],
+               T[k][:, 0:192], T.zf[:, 4 * lo + b:4 * hi:4], A_.add)
+
+        for f, done in ((catch, layer), (state, lambda c: scores(t + 1, c))):
+            for b in range(4):
+                f(0, b)
+            f(1, 0)
+            done(0)
+            for b in range(1, 4):
+                f(1, b)
+            done(1)
+
+    act(["P2"], ["ysb0"], T.ysb[:, 0:192], T.P2[:, 0:192])
     cp(["P3"], ["ysb1"], T.ysb[:, 192:384], T.P3[:, 0:192])
-    for k in range(2):
-        dma("A", "oos%d" % k, ["qx3"], [], lambda: AC.dma_start(
+    dma("S", "oc0", ["qx3a"], [], lambda: g.sync.dma_start(T.oc[:, 0:768], b8(T.qx3[:, 0:192])))
+    dma("A", "oy0", ["ysb0"], [], lambda: AC.dma_start(T.y[:, 0:192], T.ysb[:, 0:192]))
+    dma("S", "oc1", ["qx3b"], [], lambda: g.sync.dma_start(T.oc[:, 768:1536], b8(T.qx3[:, 192:384])))
+    act(["WT", "rp"], ["WN"], T.WN[:], T.WT[:, 0:C].indirect(T.rp[:, 0:24]))
+    dma("S", "oy1", ["ysb1"], [], lambda: g.sync.dma_start(T.y[:, 192:384], T.ysb[:, 192:384]))
+    for k in range(4):
+        dma("S", "oos%d" % k, ["qx3a", "qx3b"], [], lambda: g.sync.dma_start(
             T.osc[4 * k:4 * k + 4, 0:C], T.sx3[32 * k:32 * k + 4, 0:C]))
-    dma("S", "oy0", ["ysb0"], [], lambda: g.sync.dma_start(T.y[:, 0:192], T.ysb[:, 0:192]))
-    dma("A", "oy1", ["ysb1"], [], lambda: AC.dma_start(T.y[:, 192:384], T.ysb[:, 192:384]))
-    for k in range(2, 4):
-        dma("S", "oos%d" % k, ["qx3"], [], lambda: g.sync.dma_start(
-            T.osc[4 * k:4 * k + 4, 0:C], T.sx3[32 * k:32 * k + 4, 0:C]))
+    dma("A", "ool", ["WN"], [], lambda: AC.dma_start(T.ol[:], T.WN[0:128:16, :]))
     for s, c in cnt.items():
         if not any(kn.get(s, 0) >= c for kn in known.values()):
             g.wait_ge(T.sem[s], c)

from concourse.bass import IndirectOffsetOnAxis
from concourse.mybir import dt, AluOpType, ActivationFunctionType

C = 384
ROUNDS = 3
BIG = 2.0 ** 96
HOLD = 1048576
DROP = 2 ** 27
NA = 1
Q8 = "float8_e4m3fn_x4"
A_ = AluOpType
FN = ActivationFunctionType
COPY = FN.Copy
INTS = "P24 T16 T1 k24 kb kc ic pi pm k1 k3 xi xj L L2 I I2 cx cx2 r r2 oi own y2 rf b1 b2 b3 b4".split()
FLOATS = "rs RA KA wa fk".split()
PARTS = {"rs": 24, "e2": 2, "xi": 2, "X1": 2, "M": 2, "zt0": 4, "zt1": 4, "Ce": 3}
for _i in range(6):
    PARTS["C%d" % _i] = 4
PARTS["C5"] = 4 + NA
for _i in range(1, ROUNDS + 1):
    PARTS["xt%da" % _i] = PARTS["xt%db" % _i] = 4


def _ncols(a):
    return max(128, 64 * (a + 1))


SCRATCH = {"LI": ("sbuf", [128, 24 * len(INTS)], "int32"), "LF": ("sbuf", [128, 24 * len(FLOATS)], "float32")}


def _sb(name, cols, dtype):
    SCRATCH[name] = ("sbuf", [128, cols], dtype)


for _i in range(ROUNDS + 1):
    _sb("xt%d" % _i, 4 * C, "bfloat16")
    _sb("qx%d" % _i, C, Q8)
    _sb("sx%d" % _i, C, "uint8")
    SCRATCH["wd%d" % _i] = ("dram", [8, C], "float32")
for _i in range(ROUNDS):
    _sb("land%d" % _i, C, Q8)
    _sb("lans%d" % _i, C, "uint8")
    _sb("sl%d" % _i, 24, "int32")
    _sb("al%d" % _i, 24, "int32")
for _i in range(4):
    _sb("win%d" % _i, 896, "bfloat16")
    _sb("eq%d" % _i, 128, Q8)
    _sb("es%d" % _i, 128, "uint8")
for _i in range(6):
    _sb("C%d" % _i, 4 * _ncols(_i), "bfloat16")
    _sb("cq%d" % _i, _ncols(_i), Q8)
    _sb("cs%d" % _i, _ncols(_i), "uint8")
for _n, _c, _d in (
        ("Ce", 4 * C, "bfloat16"), ("ceq", C, Q8), ("ces", C, "uint8"), ("sg", NA * C, "bfloat16"),
        ("ut", 512, "bfloat16"), ("uq", 128, Q8), ("us", 128, "uint8"), ("u16q", 128, Q8), ("u16s", 128, "uint8"),
        ("vt", 512, "bfloat16"), ("vq", 128, Q8), ("vs", 128, "uint8"),
        ("wq", 512, Q8), ("wsc", 512, "uint8"), ("xh", 4 * C, "bfloat16"), ("et", 520, "bfloat16"),
        ("zt", 4 * C, "bfloat16"), ("zf", 4 * C, "bfloat16"), ("zq", C, Q8), ("zs", C, "uint8"),
        ("gt0", 512, "bfloat16"), ("gt", 512, "bfloat16"), ("gq", 128, Q8), ("gs", 128, "uint8"),
        ("zb", 520, "bfloat16"), ("junk", 24 * C, "bfloat16"),
        ("D", C, "float32"), ("mb", C, "float32"), ("kf", 8, "float32"), ("d0", C, "float32"),
        ("c2", C, "float32"), ("M", C, "float32"), ("h", C, "float32"), ("U8", 8, "int32"), ("idx", 2, "int32"),
        ("pP", 24, "uint16"), ("rp", 24, "uint16"), ("upo", 8, "uint16"), ("e1", C, "float32"), ("ru", 24, "uint16"),
        ("WT", C, "float32"), ("WN", C, "float32"), ("WS", C, "float32"),
        ("e2", C, "float32"), ("Lu", 24, "uint16"), ("TLW", 768, "float32"), ("e3", C, "float32"),
        ("e4", C, "float32"), ("tz", 24, "int32"), ("S", C, "float32"),
        ("X0", 48, "float32"), ("X1", 48, "float32"), ("so", 48, "float32"), ("tl", 24, "uint16"),
        ("ysb", C, "float32")):
    _sb(_n, _c, _d)
for _i in range(8):
    SCRATCH["P%d" % _i] = ("psum", [128, 512], "float32")
SEMAPHORES = (["sV", "sA", "sT", "sG", "loc", "lx", "ly", "lp", "lu", "lv", "lw", "ls", "oy0", "oy1", "ool", "oc0", "oc1"]
              + ["oos%d" % k for k in range(4)] + ["dw%d" % k for k in range(4)] + ["ig%d" % k for k in range(4)]
              + ["aq%d" % k for k in range(3)] + ["al%d" % k for k in range(3)])


def rank_program(g, core, T, topo):
    rank = T.rank_of(core)
    if rank is None:
        return
    nxt = T.cores[(rank + 1) % len(T.cores)]
    rid, pid = topo.addr(nxt)[:2]
    mask = topo.mask(core, nxt)
    neng = len(topo.engines(core, nxt))
    prv = T.cores[(rank - 1) % len(T.cores)]
    peng = len(topo.engines(prv, core))
    V, AC, PE = g.vector, g.scalar, g.tensor
    queue = {"V": V, "A": AC, "T": PE, "G": g, "S": g.sync}
    own = {"V": "sV", "A": "sA", "T": "sT", "G": "sG"}
    cnt, known = {}, {q: {} for q in queue}
    wr, rd = {}, {}

    def ex(keys):
        return [p for k in keys for p in (["%s.%d" % (k, i) for i in range(PARTS[k])] if k in PARTS else [k])]

    def before(q, R, W, adds=False):
        toks = []
        for k in ex(R):
            if k in wr:
                toks.append(wr[k])
        for k in ex(W):
            for t in ([wr[k]] if k in wr else []) + rd.get(k, []):
                if adds and t[2] == q:
                    continue
                toks.append(t)
        best = {}
        for t in toks:
            if known[q].get(t[0], 0) < t[1] and (t[0] not in best or best[t[0]][1] < t[1]):
                best[t[0]] = t
        keep = [t for t in best.values() if not any(o is not t and o[3].get(t[0], 0) >= t[1] for o in best.values())]
        for t in keep:
            queue[q].wait_ge(T.sem[t[0]], t[1])
            for s, c in list(t[3].items()) + [(t[0], t[1])]:
                known[q][s] = max(known[q].get(s, 0), c)

    def after(q, sem, n, R, W):
        cnt[sem] = cnt.get(sem, 0) + n
        clk = dict(known[q])
        clk[sem] = cnt[sem]
        tok = (sem, cnt[sem], q, clk)
        for k in ex(R):
            rd[k] = [t for t in rd.get(k, []) if t[0] != sem] + [tok]
        for k in ex(W):
            wr[k] = tok
            rd[k] = []

    def op(q, R, W, f, adds=False):
        before(q, R, W, adds)
        f().then_inc(T.sem[own[q]], 1)
        after(q, own[q], 1, R, W)

    def dma(q, sem, R, W, f):
        before(q, R, W)
        f().then_inc(T.sem[sem], 16)
        after(q, sem, 16, R, W)

    def b8(v):
        return v.bitcast(dt.uint8)

    def li(name, lo=0, hi=24):
        o = 24 * INTS.index(name)
        return T.LI[:, o + lo:o + hi]

    def lf(name, lo=0, hi=24):
        o = 24 * FLOATS.index(name)
        return T.LF[:, o + lo:o + hi]

    def ts(R, W, out, in0, s1, s2, op0, op1=None):
        if op1 is None:
            op("V", R, W, lambda: V.tensor_scalar(out, in0, s1, None, op0))
        else:
            op("V", R, W, lambda: V.tensor_scalar(out, in0, s1, s2, op0, op1))

    def tt(R, W, out, a, b, o):
        op("V", R, W, lambda: V.tensor_tensor(out, a, b, o))

    def cp(R, W, out, a):
        op("V", R, W, lambda: V.tensor_copy(out, a))

    def act(R, W, out, a, scale=None):
        if scale is None:
            op("A", R, W, lambda: AC.activation(out, a, COPY))
        else:
            op("A", R, W, lambda: AC.activation(out, a, COPY, scale=scale))

    def quant(R, W, q, s, t):
        op("V", R, W, lambda: V.quantize_mx(q, s, t))

    def scan(R, W, out, d0, d1, init, o0, o1):
        op("V", R, W, lambda: V.tensor_tensor_scan(out, d0, d1, init, o0, o1))

    def mm(R, W, out, lq, ls_, rq, rs_, start=True, stop=True):
        op("T", R, W, lambda: PE.matmul_mx(out, lq, ls_, rq, rs_, start, stop), not start)

    def arrives(key, sem, n):
        cnt[sem] = n
        wr[key] = (sem, n, "-", {})

    for t in range(ROUNDS):
        arrives("land%d" % t, "aq%d" % t, 2 * peng)
        arrives("al%d" % t, "al%d" % t, peng)

    dma("S", "lx", [], ["xt0a"], lambda: g.sync.dma_start(T.xt0[:, 0:768], T.x[:, 0:768]))
    dma("A", "lu", [], ["ut"], lambda: AC.dma_start(T.ut[:], T.u[:]))
    dma("A", "ly", [], ["xt0b"], lambda: AC.dma_start(T.xt0[:, 768:1536], T.x[:, 768:1536]))
    dma("S", "lp", [], ["pi"], lambda: g.sync.dma_start(li("pi"), T.p[:]))

    op("G", [], ["P24"], lambda: g.iota(li("P24"), [[0, 24]], 0, 1))
    op("G", [], ["D"], lambda: g.iota(T.D[:], [[0, 24], [1, 16]], 0, 0, allow_small_or_imprecise_dtypes=True))
    op("G", [], ["U8"], lambda: g.iota(T.U8[:], [[16, 8]], 0, 0))
    op("G", [], ["T16"], lambda: g.iota(li("T16"), [[16, 24]], 0, 0))
    op("G", [], ["T1"], lambda: g.iota(li("T1"), [[1, 24]], 0, 0))
    op("V", [], ["zb"], lambda: V.memset(T.zb[:], 0.0))
    op("V", [], ["rs"], lambda: V.memset(lf("rs"), 0.0))
    op("V", [], ["X0"], lambda: V.memset(T.X0[:], 0.0))
    ts(["P24"], ["k24"], li("k24"), li("P24"), 15, None, A_.bitwise_and)
    ts(["P24"], ["idx"], T.idx[:, 0:1], li("P24", 0, 1), 4, None, A_.logical_shift_right)
    cp(["k24"], ["kf"], T.kf[:, 0:1], li("k24", 0, 1))
    op("G", ["zb"], ["et"], lambda: g.affine_select(T.et[:], T.zb[:, 0:520], [[1, 520]], A_.not_equal, 1.0, -4, -4))
    op("G", ["zb"], ["gt0"], lambda: g.affine_select(
        T.gt0[:], T.zb[:, 0:512], [[16, 8], [0, 64]], A_.is_gt, 1.0, 0, -1))
    op("G", ["gt0"], ["gt"], lambda: g.affine_select(T.gt[:], T.gt0[:], [[16, 8], [0, 64]], A_.is_ge, 0.0, 15, -1))
    for a in range(6):
        lo, hi = 256 * a, max(512, 256 * a + 256)
        act(["zb"], ["C%d" % a], T["C%d" % a][:, lo:hi], T.zb[:, 0:hi - lo])
    act(["zb"], ["Ce.0"], T.Ce[:, 0:512], T.zb[:, 0:512])
    ts(["D", "kf"], ["mb"], T.mb[:], T.D[:], T.kf[:, 0:1], BIG, A_.not_equal, A_.mult)
    ts(["D", "kf"], ["d0"], T.d0[:], T.D[:], T.kf[:, 0:1], BIG, A_.is_equal, A_.mult)
    cp(["U8"], ["upo"], T.upo[:], T.U8[:])
    tt(["T16", "k24"], ["ic"], li("ic"), li("T16"), li("k24"), A_.add)
    op("V", [], ["d0"], lambda: V.memset(T.d0[:, 0:C:16], BIG))
    ts(["k24"], ["kb"], li("kb"), li("k24"), HOLD, None, A_.mult)
    ts(["ic"], ["pm"], li("pm"), li("ic"), 1024, 524288, A_.mult, A_.add)
    ts(["k24"], ["k1"], li("k1"), li("k24"), 24, None, A_.mult)
    tt(["pm", "pi"], ["wa"], lf("wa"), li("pm"), li("pi"), A_.add)
    dma("S", "dw0", ["wa"], ["wd0"], lambda: g.sync.dma_start(T.wd0[:], lf("wa")))
    tt(["kb", "T16"], ["kc"], li("kc"), li("T16"), li("kb"), A_.add)
    tt(["k1", "T1"], ["k3"], li("k3"), li("k1"), li("T1"), A_.add)
    ts(["kb"], ["fk"], lf("fk"), li("kb"), -1, 15 * HOLD + 511, A_.mult, A_.add)
    ts(["kc"], ["KA"], lf("KA"), li("kc"), -1 - 15 * HOLD, None, A_.add)
    cp(["k3"], ["pP"], T.pP[:], li("k3"))
    ts(["mb"], ["c2"], T.c2[:], T.mb[:], (DROP + HOLD) / BIG, -float(DROP), A_.mult, A_.add)
    quant(["ut"], ["uq"], T.uq[:, 0:128], T.us[:, 0:128], T.ut[:])
    cp(["uq", "upo"], ["u16q"], T.u16q[:, 0:128].bitcast(dt.uint32),
       T.uq[:, 0:128].bitcast(dt.uint32).indirect(T.upo[:, 0:8]))
    act(["uq", "upo"], ["u16s"], T.u16s[:, 0:128], T.us[:, 0:128].indirect(T.upo[:, 0:8]))
    dma("S", "lw", ["xt0a", "xt0b"], ["wq"], lambda: g.sync.dma_start(b8(T.wq[:, 0:512]), T.wc[:]))
    dma("S", "ls", [], ["wsc"], lambda: g.sync.dma_start(T.wsc[:, 0:512], T.ws[:]))
    dma("S", "lv", [], ["vt"], lambda: g.sync.dma_start(T.vt[:], T.v[:]))

    def spread(i):
        dma("G", "ig%d" % i, ["wd%d" % i, "idx"], ["WT"], lambda: g.indirect_dma_start(
            T.WT[:], None, T["wd%d" % i][:], IndirectOffsetOnAxis(ap=T.idx[:, 0:1], axis=0), bounds_check=7))

    spread(0)

    def scores(t, c):
        qx, sx, k = T["qx%d" % t], T["sx%d" % t], "P%d" % (2 + c)
        lo, hi = 192 * c, 192 * c + 192
        kq = "qx%d%s" % (t, "ab"[c])
        quant(["xt%d%s" % (t, "ab"[c])], [kq], qx[:, lo:hi], sx[:, lo:hi], T["xt%d" % t][:, 4 * lo:4 * hi])
        if t < ROUNDS:
            mm(["u16q", "u16s", kq], [k], T[k][:, 0:192], T.u16q[:, 0:128], T.u16s[:, 0:128], qx[:, lo:hi], sx[:, lo:hi])
            if c == 0:
                if t == 0:
                    act(["zb"], ["Ce.1"], T.Ce[:, 512:1024], T.zb[:, 0:512])
                act([k], ["S0", "turn0"], T.S[:, 0:192], T[k][:, 0:192])
                if t == 0:
                    act(["zb"], ["Ce.2"], T.Ce[:, 1024:1536], T.zb[:, 0:512])
        else:
            mm(["vq", kq], [k], T[k][:, 0:192], T.vq[:, 0:128], T.vs[:, 0:128], qx[:, lo:hi], sx[:, lo:hi])

    for t in range(ROUNDS):
        xt, qx, sx = T["xt%d" % t], T["qx%d" % t], T["sx%d" % t]
        kx = ["xt%da" % t, "xt%db" % t]
        kq = "qx%d" % t

        def half(b):
            act(kx, ["winx%d" % b], T["win%d" % b][:, 0:C], xt[:, b:4 * C:4], 2.0 ** -6)

        if t == 0:
            scores(0, 0)
            scores(0, 1)
        before("G", [kq + "a", kq + "b"], [])
        g.remote_dma(b8(T["land%d" % t][:, 0:C]), b8(qx[:, 0:C]), T.sem["aq%d" % t], T.sem.loc, pid, rid, mask)
        g.remote_dma(T["lans%d" % t][:, 0:C], sx[:, 0:C], T.sem["aq%d" % t], T.sem.loc, pid, rid, mask)
        cnt["loc"] = cnt.get("loc", 0) + 2 * neng
        if t == 0:
            for b in range(4):
                quant(["et"], ["eq%d" % b], T["eq%d" % b][:, 0:128], T["es%d" % b][:, 0:128], T.et[:, 4 - b:516 - b])
        tt(["P2", "mb", "turn0"], ["M.0"], T.M[:, 0:192], T.P2[:, 0:192], T.mb[:, 0:192], A_.add)
        tt(["P3", "mb"], ["M.1", "turn1"], T.M[:, 192:384], T.P3[:, 0:192], T.mb[:, 192:384], A_.add)
        act(["P3", "turn1"], ["S1"], T.S[:, 192:384], T.P3[:, 0:192])
        scan(["d0", "M"], ["h"], T.h[:], T.d0[:], T.M[:], BIG, A_.add, A_.min)

        for n in range(NA):
            b = 3 - n
            w = 16 * (20 + b)
            op("A", ["S0", "S1", "h"], ["sg%d" % n], lambda: AC.activation(
                T.sg[:, C * n:C * n + w], T.S[:, 0:w], FN.Sign, bias=T.h[:, w + 15:w + 16], scale=-1.0))
            op("A", ["sg%d" % n], ["C5.%d" % (4 + n), "rs.%d" % (20 + b)], lambda: AC.activation(
                T.C5[:, b:4 * w:4], T.sg[:, C * n:C * n + w], FN.Relu, accum_out=lf("rs", 20 + b, 21 + b)))

        def compare(a):
            Ct = T["C%d" % a]
            mine = [b for b in (3, 2, 1, 0) if a < 5 or b < 4 - NA]
            for b in mine + [b for b in (3, 2, 1, 0) if b not in mine]:
                w = 16 * (4 * a + b) + 16
                lo = 0 if b in mine else w - 16
                ts(["S0", "S1", "h"], ["C%d.%d" % (a, b)], Ct[:, 4 * lo + b:4 * w:4], T.S[:, lo:w], T.h[:, w - 1:w], None,
                   A_.is_lt)
            for b in mine:
                j = 4 * a + b
                if j:
                    op("A", ["C%d.%d" % (a, b)], ["rs.%d" % j, "junk%d" % j], lambda: AC.activation(
                        T.junk[:, C * j:C * j + 16 * j], Ct[:, b:64 * j:4], COPY, accum_out=lf("rs", j, j + 1)))

        def count(a, start=False, stop=False):
            n = _ncols(a)
            quant(["C%d" % a], ["cq%d" % a], T["cq%d" % a][:, 0:n], T["cs%d" % a][:, 0:n], T["C%d" % a][:, 0:4 * n])
            mm(["gq", "cq%d" % a], ["P1"], T.P1[:, 0:n], T.gq[:, 0:128], T.gs[:, 0:128],
               T["cq%d" % a][:, 0:n], T["cs%d" % a][:, 0:n], start, stop)

        compare(5)
        if t == 0:
            quant(["gt"], ["gq"], T.gq[:, 0:128], T.gs[:, 0:128], T.gt[:])
        compare(4)
        count(5, start=True)
        compare(3)
        count(4)
        for c in range(2):
            lo, hi = 192 * c, 192 * c + 192
            tt(["h", "P%d" % (2 + c), "S%d" % c], ["Ce.%d" % (2 * c), "eqs%d" % c] + (["Ce.1"] if c == 0 else []),
               T.Ce[:, 4 * lo:4 * hi:4], T.h[:, lo:hi], T["P%d" % (2 + c)][:, 0:192], A_.is_equal)
        count(3)
        compare(2)
        quant(["Ce", "eqs0", "eqs1"], ["ceq"], T.ceq[:, 0:C], T.ces[:, 0:C], T.Ce[:])
        mm(["gq", "ceq"], ["P1"], T.P1[:, 0:C], T.gq[:, 0:128], T.gs[:, 0:128], T.ceq[:, 0:C], T.ces[:, 0:C], False, False)
        compare(1)
        count(2)
        compare(0)
        count(1)
        count(0, stop=True)
        k = "rp" if t else "pP"
        act(["WT", k], ["WN"], T.WN[:], T.WT[:, 0:C].indirect(T[k][:, 0:24]))
        for c in range(2):
            act(["zb"], ["TLW"] if c else ["TLWa"], T.TLW[:, 384 * c:384 * c + 384], T.zb[:, 0:384])
        for b in range(4):
            half(b)
            if t == 0:
                act(["zb"], ["gap%d" % b], T["win%d" % b][:, 384:512], T.zb[:, 0:128])
        act(kx, ["xh"], T.xh[:], xt[:], 2.0 ** -6)
        for b in range(4):
            mm(["eq%d" % b, "land%d" % t], ["P%d" % (4 + b)], T["P%d" % (4 + b)][:, 0:C], T["eq%d" % b][:, 0:128],
               T["es%d" % b][:, 0:128], T["land%d" % t][:, 0:C], T["lans%d" % t][:, 0:C])
        for b in range(4):
            act(["P%d" % (4 + b)], ["wind%d" % b], T["win%d" % b][:, 512:896], T["P%d" % (4 + b)][:, 0:C], 2.0 ** -6)
        tt(["KA", "rs"], ["RA"], lf("RA"), lf("KA"), lf("rs"), A_.subtract)
        scan(["c2", "P1"], ["e1"], T.e1[:], T.c2[:], T.P1[:, 0:C], 0.0, A_.add, A_.max)
        tt(["e1", "RA"], ["rf"], li("rf"), T.e1[:, 15:C:16], lf("RA"), A_.add)
        cp(["rf"], ["ru"], T.ru[:], li("rf"))
        cp(["ru", "WN"], ["WS"], T.WS[:, 0:C].indirect(T.ru[:, 0:24]), T.WN[:])
        scan(["c2", "WS"], ["e2.0"], T.e2[:, 0:192], T.c2[:, 0:192], T.WS[:, 0:C:2], 0.0, A_.add, A_.max)
        scan(["c2", "WS"], ["e2.1"], T.e2[:, 192:384], T.c2[:, 0:192], T.WS[:, 1:C:2], 0.0, A_.add, A_.max)
        cp(["e2"], ["xi.0"], li("xi"), T.e2[:, 15:C:16])
        cp(["e2"], ["xi.1"], li("xj"), T.e2[:, 15:C:16])
        ts(["xi"], ["L"], li("L", 0, 48), li("xi", 0, 48), 1023, None, A_.bitwise_and)
        ts(["xi"], ["I"], li("I", 0, 36), li("xi", 0, 36), 10, 511, A_.logical_shift_right, A_.bitwise_and)
        tt(["L", "I"], ["cx"], li("cx", 0, 36), li("L", 12, 48), li("I", 0, 36), A_.subtract)
        tt(["L"], ["X1.0"], T.X1[:, 0:48:2], li("L", 12, 36), li("L", 0, 24), A_.subtract)
        ts(["cx"], ["r"], li("r", 0, 36), li("cx", 0, 36), -191.5, 1.0 / 384, A_.add, A_.mult)
        cp(["L"], ["X1.1"], T.X1[:, 1:48:2], li("L"))
        tt(["r"], ["X0"], T.X0[:, 1:48:2], li("r", 0, 24), li("r", 12, 36), A_.is_equal)
        scan(["X0", "X1"], ["so"], T.so[:], T.X0[:], T.X1[:], 0.0, A_.mult, A_.add)
        cp(["so"], ["Lu"], T.Lu[:], T.so[:, 1:48:2])
        kw = "wd%d" % (t + 1)
        if t == ROUNDS - 1:
            cp(["so"], ["wa"], lf("wa"), T.so[:, 1:48:2])
            dma("S", "dw%d" % (t + 1), ["wa"], [kw], lambda: g.sync.dma_start(T[kw][:], lf("wa")))
        cp(["Lu", "WS"], ["TLW", "TLWa"], T.TLW[:, 0:768].indirect(T.Lu[:, 0:12]), T.WS[:, 0:C:2])
        cp(["Lu", "WS"], ["TLW", "TLWa"], T.TLW[:, 0:768].indirect(T.Lu[:, 12:24]), T.WS[:, 1:C:2])
        scan(["c2", "TLW"], ["e3"], T.e3[:], T.c2[:], T.TLW[:, 384:768], 0.0, A_.add, A_.max)
        ksl = "sl%d" % t
        ts(["e3", "fk"], [ksl], T[ksl][:], T.e3[:, 15:C:16], lf("fk", 0, 1), 2.0 ** -10, A_.subtract, A_.mult)
        before("G", [ksl], [])
        g.remote_dma(T["al%d" % t][:], T[ksl][:], T.sem["al%d" % t], T.sem.loc, pid, rid, mask)
        cnt["loc"] += neng
        scan(["c2", "TLW", "TLWa"], ["e4"], T.e4[:], T.c2[:], T.TLW[:, 0:384], 0.0, A_.add, A_.max)
        if t < ROUNDS - 1:
            ts(["xi"], ["y2"], li("y2"), li("xi"), 1023 * 1024, None, A_.bitwise_and)
        cp(["e4"], ["oi"], li("oi"), T.e4[:, 15:C:16])
        if t < ROUNDS - 1:
            tt(["so", "y2"], ["wa"], lf("wa"), T.so[:, 1:48:2], li("y2"), A_.add)
        ts(["oi"], ["own"], li("own"), li("oi"), 10, 511, A_.logical_shift_right, A_.bitwise_and)
        if t < ROUNDS - 1:
            dma("S", "dw%d" % (t + 1), ["wa"], [kw], lambda: g.sync.dma_start(T[kw][:], lf("wa")))
        spread(t + 1)
        ts(["rf"], ["b1"], li("b1"), li("rf"), 31, None, A_.bitwise_and)
        ts(["rf"], ["b2"], li("b2"), li("rf"), 5, None, A_.logical_shift_right)
        ts(["b1"], ["b3"], li("b3"), li("b1"), 12, None, A_.mult)
        tt(["b3", "b2"], ["b4"], li("b4"), li("b3"), li("b2"), A_.add)
        cp(["b4"], ["rp"], T.rp[:], li("b4"))
        if t == 0:
            quant(["vt"], ["vq"], T.vq[:, 0:128], T.vs[:, 0:128], T.vt[:])
        tt(["own", "al%d" % t], ["tz"], T.tz[:], li("own"), T["al%d" % t][:], A_.add)
        cp(["tz"], ["tl"], T.tl[:], T.tz[:])
        banks = [[2, 3, 4, 5], [6, 7, 0, 1]]

        def catch(c, b):
            lo, hi = 192 * c, 192 * c + 192
            tt(["winx%d" % b, "gap%d" % b, "wind%d" % b, "xh", "tl"], ["zt%d.%d" % (c, b)],
               T.zt[:, 4 * lo + b:4 * hi:4], T["win%d" % b][:, 0:896].indirect(T.tl[:, 12 * c:12 * c + 12]),
               T.xh[:, 4 * lo + b:4 * hi:4], A_.add)

        def layer(c):
            lo, hi = 192 * c, 192 * c + 192
            quant(["zt%d" % c], ["zq%d" % c], T.zq[:, lo:hi], T.zs[:, lo:hi], T.zt[:, 4 * lo:4 * hi])
            act(["zt%d" % c], ["zf%d" % c], T.zf[:, 4 * lo:4 * hi], T.zt[:, 4 * lo:4 * hi], 32.0)
            for b in range(4):
                k = "P%d" % banks[c][b]
                mm(["wq", "wsc", "zq%d" % c], [k], T[k][:, 0:192], T.wq[:, 128 * b:128 * b + 128],
                   T.wsc[:, 128 * b:128 * b + 128], T.zq[:, lo:hi], T.zs[:, lo:hi])

        def state(c, b):
            lo, hi = 192 * c, 192 * c + 192
            k = "P%d" % banks[c][b]
            tt([k, "zf%d" % c], ["xt%d%s.%d" % (t + 1, "ab"[c], b)], T["xt%d" % (t + 1)][:, 4 * lo + b:4 * hi:4],
               T[k][:, 0:192], T.zf[:, 4 * lo + b:4 * hi:4], A_.add)

        for f, done in ((catch, layer), (state, lambda c: scores(t + 1, c))):
            for b in range(4):
                f(0, b)
            f(1, 0)
            done(0)
            for b in range(1, 4):
                f(1, b)
            done(1)

    act(["P2"], ["ysb0"], T.ysb[:, 0:192], T.P2[:, 0:192])
    cp(["P3"], ["ysb1"], T.ysb[:, 192:384], T.P3[:, 0:192])
    dma("S", "oc0", ["qx3a"], [], lambda: g.sync.dma_start(T.oc[:, 0:768], b8(T.qx3[:, 0:192])))
    dma("A", "oy0", ["ysb0"], [], lambda: AC.dma_start(T.y[:, 0:192], T.ysb[:, 0:192]))
    dma("S", "oc1", ["qx3b"], [], lambda: g.sync.dma_start(T.oc[:, 768:1536], b8(T.qx3[:, 192:384])))
    act(["WT", "rp"], ["WN"], T.WN[:], T.WT[:, 0:C].indirect(T.rp[:, 0:24]))
    dma("S", "oy1", ["ysb1"], [], lambda: g.sync.dma_start(T.y[:, 192:384], T.ysb[:, 192:384]))
    for k in range(4):
        dma("S", "oos%d" % k, ["qx3a", "qx3b"], [], lambda: g.sync.dma_start(
            T.osc[4 * k:4 * k + 4, 0:C], T.sx3[32 * k:32 * k + 4, 0:C]))
    dma("A", "ool", ["WN"], [], lambda: AC.dma_start(T.ol[:], T.WN[0:128:16, :]))
    for s, c in cnt.items():
        if not any(kn.get(s, 0) >= c for kn in known.values()):
            g.wait_ge(T.sem[s], c)
